import numpy as np, ml_dtypes
CORES = [6,15,38,47]
N = 4
import mx_ref
BF = ml_dtypes.bfloat16
def pick(q, e):
    c = np.concatenate([q[0].reshape(128, -1, 4), np.zeros((128, 1, 4), np.uint8)], axis=1); s = np.concatenate([q[1], np.ones((16, 1), np.uint8)], axis=1)
    return (np.ascontiguousarray(c[:, e].reshape(128, -1)), np.ascontiguousarray(s[:, e]))
def join(*qs):
    return (np.concatenate([q[0] for q in qs], axis=1), np.concatenate([q[1] for q in qs], axis=1))
def put(q, e, v):
    c, s = q[0].reshape(128, -1, 4).copy(), q[1].copy(); c[:, e] = v[0].reshape(128, -1, 4); s[:, e] = v[1]
    return (c.reshape(128, -1), s)
def pk(c, s):
    return (np.ascontiguousarray(c), mx_ref.live(s))
def emit(q):
    return q[0], q[1]
def tile(rs):
    return np.stack(rs, axis=2).reshape(128, -1).astype(BF)
def cut(t, i, w=512):
    return t[:, w * i:w * i + w]
def f(rng, *shape):
    return mx_ref.flush((rng.standard_normal(shape, dtype=np.float32) * np.exp2(rng.integers(-2, 3, shape[:-1] + (1,)))).astype(BF))
def wide(rng, *shape, cols=0):
    v = rng.standard_normal(shape, dtype=np.float32) * np.exp2(rng.integers(-12, 13, shape)).astype(np.float32)
    if cols: v *= np.repeat(np.exp2(rng.integers(-cols, cols + 1, shape[:-2] + (1, shape[-1] // 4))) * (rng.random(shape[:-2] + (1, shape[-1] // 4)) > 0.0625), 4, axis=-1).astype(np.float32)
    return mx_ref.flush(v.astype(BF))
T, CAPP, CAPR = 224, 128, 48
def same(t):
    return np.stack([np.concatenate([t, np.zeros((128, 512 - t.shape[1]), BF)], axis=1)] * N)
def bf(t):
    return np.asarray(t, np.float32).astype(BF)
def sized(rng, *shape):
    return 1 + rng.random(shape)
def signs(rng, *shape):
    return 1 - 2 * rng.integers(0, 2, shape)
def setup_inputs(rng):
    return {"x": f(rng, N, 128, 4 * T), "rt": same(f(rng, 128, 4 * N)), "w": f(rng, N, 128, 2048), "u": same(f(rng, 128, 4)), "v": f(rng, N, 128, 512)}
def planted(rng, a, b, own=1.0, off=1.0, way=1):
    d = setup_inputs(rng)
    at = np.arange(128) // (128 // N)
    big, mid = at[None, :, None] == a[:, None, :], at[None, :, None] == b[:, None, :]
    k = np.where(big, 16.0, np.where(mid, 4.0, 1.0))[..., None]
    g = np.where((big | mid)[..., None], 1, signs(rng, N, 128, T, 4))
    d["x"] = bf(sized(rng, N, 128, T, 4) * k * g).reshape(N, 128, 4 * T)
    d["rt"] = same(bf(sized(rng, 128, N, 4) * (at[:, None] == np.arange(N))[..., None]).reshape(128, 4 * N))
    d["w"] = bf(sized(rng, N, 128, 2048) * signs(rng, N, 128, 2048) * np.where(at == np.arange(N)[:, None], own, off)[..., None])
    d["u"] = same(bf(way * sized(rng, 128, 4)))
    return d
def setup_inputs_crowd(rng):
    a, b = np.zeros((N, T), int), np.zeros((N, T), int)
    for s in range(N):
        h, k = (s + (0, 1, 1)[s % 3]) % N, (s + (1, 0, 2)[s % 3]) % N
        rest = rng.permutation(np.array([e for e in range(N) if e not in (h, k)]))
        m, n = rest[np.arange(T) % rest.size], rest[np.arange(1, T + 1) % rest.size]
        p = rng.permutation(T)
        p[:CAPP + 16] = np.sort(p[:CAPP + 16])
        m[:CAPP + 16] = h
        m[CAPP + 16:CAPP + 16 + CAPR] = k
        n[np.concatenate([np.arange(CAPP + 16 + CAPR, T), np.arange(CAPP)])[:CAPP - CAPR]] = k
        a[s, p], b[s, p] = m, n
    return planted(rng, a, b, own=2.0 ** -4, way=-2.0 ** 24)
def setup_inputs_second(rng):
    a, b = np.zeros((N, T), int), np.zeros((N, T), int)
    one, i = int(rng.integers(0, N)), np.arange(T)
    half, last = CAPP // 2, CAPP + CAPP // 2 + 16
    for s in range(N):
        g = rng.permutation(N)
        h, k, rest = g[0], g[1], g[2:]
        m, n = rest[i % rest.size], rest[(i + 1) % rest.size]
        if s == one:
            m[:] = h
            n = g[1 + i % (N - 1)]
        else:
            m[:last] = h
            n[half:last] = k
        turn = (i + rng.integers(0, 2)) % 2 == 1
        p = rng.permutation(T)
        p[:last] = np.sort(p[:last])
        a[s, p], b[s, p] = np.where(turn, m, n), np.where(turn, n, m)
    return planted(rng, a, b, own=2.0 ** 4, way=-1)
def setup_inputs_ties(rng):
    kind = np.stack([rng.permutation(T) % N for s in range(N)])
    e = rng.integers(2, N, (N, T))
    a = np.where(kind == 0, 0, e)
    b = np.where(kind == 0, e, np.where(kind == 1, 0, e ^ 1))
    d = planted(rng, a, b)
    d["rt"][:, :, 4:8] = d["rt"][:, :, :4]
    d["w"][1::2] = d["w"][::2]
    d["w"][:2, :, :4] = 0
    d["w"][1, 128 // N, 0] = BF(4)
    return d
def setup_inputs_zero(rng):
    a = rng.integers(0, N, (N, T))
    b = (a + rng.integers(1, N, (N, T))) % N
    d = planted(rng, a, b, way=-1)
    at, late = np.arange(128) // (128 // N), np.arange(128) % (128 // N) >= 128 // N // 2
    kind = np.stack([rng.permutation(T) % 4 for s in range(N)])
    low = (at[None, :, None] == a[:, None, :]) & (kind % 2 == 1)[:, None, :] | (at[None, :, None] == b[:, None, :]) & (kind >= 2)[:, None, :]
    t = d["x"].astype(np.float32).reshape(N, 128, T, 4)
    d["x"] = bf(np.where(late[None, :, None, None], np.abs(t) * np.where(low, -1, 1)[..., None], t)).reshape(N, 128, 4 * T)
    d["rt"] = bf(d["rt"].astype(np.float32) * ~late[None, :, None])
    d["w"] = bf(np.abs(d["w"].astype(np.float32)) * ((at == np.arange(N)[:, None]) & late)[..., None])
    return d
def setup_inputs_spread(rng):
    return {**setup_inputs(rng), "x": wide(rng, N, 128, 4 * T, cols=6)}
def check_inputs(d):
    b = []
    for k in ("x", "rt", "w", "u", "v"):
        t = np.abs(d[k].astype(np.float32))
        if not (np.isfinite(t).all() and ((t == 0) | (t >= 2.0 ** -30) & (t <= 2.0 ** 30)).all()): b.append("a value of " + k)
    for k, n in (("rt", N), ("u", 1)):
        t = d[k].astype(np.float32)
        if (t[:, :, 4 * n:] != 0).any(): b.append(k + " has numbers behind its first columns")
        if (t != t[:1]).any(): b.append(k + " isn't the same on all ranks")
    return b
def reference(x, rt, w, u, v):
    q, a, b = [], [], []
    for s in range(N):
        q.append(mx_ref.quantize(np.ascontiguousarray(x[s])))
        z = mx_ref.matmul(mx_ref.quantize(np.ascontiguousarray(rt[s])), q[s])[:N] + np.float32(0)
        o = np.argsort(-z, axis=0, kind="stable")
        a.append(o[0])
        b.append(o[1])
    took = [[np.flatnonzero((a[s] == e) | (b[s] == e))[:CAPP] for e in range(N)] for s in range(N)]
    good = np.full((N, N, T), -np.inf, np.float32)
    made = []
    for e in range(N):
        t = join(*[pick(q[s], np.concatenate([took[s][e], np.full(CAPP - took[s][e].size, -1)])) for s in range(N)])
        rs = [mx_ref.matmul(mx_ref.quantize(np.ascontiguousarray(cut(w[e], i))), t) for i in range(4)]
        made.append(mx_ref.quantize(tile([np.maximum(k, np.float32(0)) * np.float32(0.0625) for k in rs])))
        z = mx_ref.matmul(mx_ref.quantize(np.ascontiguousarray(u[e])), made[e])[0] + np.float32(0)
        for s in range(N): good[s, e, took[s][e]] = z[s * CAPP:s * CAPP + took[s][e].size]
    every = join(*made)
    oc, osc = np.zeros((N, 128, 4 * T), np.uint8), np.zeros((N, 16, T), np.uint8)
    wn, y = np.zeros((N, 1, T), np.float32), np.zeros((N, 128, T), np.float32)
    for s in range(N):
        ga, gb = good[s, a[s], np.arange(T)], good[s, b[s], np.arange(T)]
        win = np.where(ga >= gb, a[s], b[s])
        none = np.maximum(ga, gb) == -np.inf
        wn[s, 0] = np.where(none, -100, -1 - win)
        at = np.full(T, -1)
        for e in range(N):
            home = np.flatnonzero((win == e) & ~none)[:CAPR]
            wn[s, 0, home] = e
            at[home] = (e * N + s) * CAPP + np.searchsorted(took[s][e], home)
        z = pick(every, at)
        oc[s], osc[s] = emit(z)
        y[s] = mx_ref.matmul(mx_ref.quantize(np.ascontiguousarray(v[s])), z)
    return {"oc": oc, "osc": osc, "wn": wn, "y": y}

@@ -1,0 +1,539 @@
+from concourse.mybir import dt, AluOpType as A, ActivationFunctionType as F
+
+
+def _buffers():
+    d = {"dg": ("dram", [384, 1], "float32"), "ps": ("psum", [128, 4096], "float32")}
+    kinds = {
+        "bfloat16": "xt 1088 rtt 512 wt 2048 ut 512 vt 512 hb 2112 rst 256 one 256 tok 480 a1 256 a2 256 cc 256 mm 256 nn 256 "
+                    "pp 256 tp 256 el 1088 lt 640 wa 256 wat 256 m2 256 n2 256 rc 256 rtr 256 "
+                    "tabw 512 tab 576 vp 64 bt 588 sc 588 rsl 196",
+        "float32": "ysb 224 sf 40 zero 16 tokf 480 kp 60 pe 128 pp2 128 ka 64 kb 64 kz 64 kr 64 kv 64 kv2 64 kv3 64 mab 128 pab 120 "
+                   "t1 120 xn 40 xp 40 wl 40 xn1 10 xp1 10 wl1 10 tk 64 abe 128 v2 64 pab2 128 t2 128 ae 64 be 64 de 64 qs 4 "
+                   "gt 528 gtt 528 gab 256 x4 64 qo 128 own 128 gab2 256 isa 256 lab 256 lab2 320 lt1 256 lt0 256 h1 64 hm 64 xz 64 "
+                   "z1 64 z2 64 z3 64 zn 16 zp 16 zl 14 w1 64 w2 64 w3 64 w4 64 wnw 256 wnf 256",
+        "uint16": "sl 20 ul 8 off1 30 off2 40 off2a 10 off3 32 offl 24 off5 14 ls 16 la 12",
+        "int32": "si 8",
+    }
+    for t, text in kinds.items():
+        w = text.split()
+        for name, n in zip(w[::2], w[1::2]):
+            d[name] = ("sbuf", [128, int(n)], t)
+    d["cb"] = d.pop("one")[:1] + ([128, 640], "bfloat16")
+    w = "xq 272 rq 128 rr 288 wq 512 uq 128 ur 128 vq 128 xs 512 xl 384 hq 384 hs 144 zq 288 z 224".split()
+    for name, n in zip(w[::2], w[1::2]):
+        d[name] = ("sbuf", [128, int(n)], "float8_e4m3fn_x4")
+        d[name + "s"] = ("sbuf", [128, int(n)], "uint8")
+    return d
+
+
+SCRATCH = _buffers()
+SEMAPHORES = ["v", "s", "t", "p", "dx", "dx2", "dr", "dw", "du", "dv", "dgt", "dgo", "out", "sent", "qa", "ha"] \
+    + ["xa%d" % i for i in range(3)] + ["ar%d" % i for i in range(3)]
+FAR = 4096
+WAKE, CYC = 0.12, 0.00083
+
+
+def _o(name, a=0, z=None, step=1):
+    return ("@", name, a, SCRATCH[name][1][1] if z is None else z, step, None, None, None)
+
+
+def _cast(o, how):
+    return o[:5] + (how,) + o[6:]
+
+
+def _ind(o, off):
+    return o[:6] + (off, o[7])
+
+
+def _part(o, p, n=32):
+    return o[:7] + ((p, p + n),)
+
+
+def _keys(o):
+    if o[1] == "ps":
+        return [("ps", b) for b in range(o[2] // 512, (o[3] - 1) // 512 + 1)]
+    blocks = range(o[7][0] // 32, (o[7][1] - 1) // 32 + 1) if o[7] else range(4)
+    return [(o[1], c, b) for c in range(o[2], o[3], o[4]) for b in blocks]
+
+
+def _isop(x):
+    return isinstance(x, tuple) and len(x) == 8 and x[0] == "@"
+
+
+def _width(o):
+    return 16 * (o[6][3] - o[6][2]) if o[6] else len(range(o[2], o[3], o[4]))
+
+
+def _cost(name, args):
+    out, n = args[0], _width(args[0])
+    if name == "mx":
+        return (n + 16) * CYC
+    if name == "q":
+        return .012 + .00088 * n
+    ops = [a for a in args if _isop(a)]
+    if name == "pb":
+        return .14 + 4 * n * CYC
+    if name == "iota":
+        return .13 + 2 * n * CYC
+    if name == "act":
+        return .065 + n * CYC * (1.5 if args[1][6] else 1)
+    if out[6]:
+        return .05 + 3 * n * CYC
+    if any(a[6] for a in ops):
+        return .05 + 1.6 * n * CYC
+    two = all(SCRATCH[a[1]][2] in ("bfloat16", "uint16") for a in ops if _width(a) > 1)
+    return max(64, n * (2 if name == "tt" else .5 if two else 1)) * CYC
+
+
+def _order(ops):
+    n = len(ops)
+    prio = [0.0] * n
+    for i in range(n - 1, -1, -1):
+        prio[i] += ops[i]["cost"] + ops[i]["lat"]
+        for d in ops[i]["deps"]:
+            prio[d] = max(prio[d], prio[i] + WAKE)
+    need = [len(o["deps"]) for o in ops]
+    succ = [[] for o in ops]
+    for i, o in enumerate(ops):
+        for d in o["deps"]:
+            succ[d].append(i)
+    ready, fin, free = [0.0] * n, [0.0] * n, {}
+    can, lists = {}, {}
+
+    def release(i):
+        q = ops[i]["q"]
+        if q is None:
+            finish(i, ready[i])
+        else:
+            can.setdefault(q, []).append(i)
+
+    def finish(i, start):
+        fin[i] = start + ops[i]["cost"] + ops[i]["lat"]
+        for j in succ[i]:
+            ready[j] = max(ready[j], fin[i] + (WAKE if ops[j]["q"] else 0))
+            need[j] -= 1
+            if need[j] == 0:
+                release(j)
+    for i in range(n):
+        if not ops[i]["deps"]:
+            release(i)
+    while True:
+        best = None
+        for q, c in can.items():
+            if not c:
+                continue
+            t = free.get(q, 0.0)
+            m = min(max(t, ready[i]) for i in c)
+            pick = max((i for i in c if max(t, ready[i]) <= m + 1e-9), key=lambda i: prio[i])
+            for d in sorted(c, key=lambda i: -prio[i]):
+                e = max(t, ready[d])
+                if prio[d] > prio[pick] and e - m < m + ops[pick]["cost"] - e:
+                    pick, m = d, e
+                    break
+            if best is None or m < best[0]:
+                best = (m, q, pick)
+        if best is None:
+            break
+        m, q, i = best
+        can[q].remove(i)
+        lists.setdefault(q, []).append(i)
+        free[q] = m + ops[i]["cost"]
+        finish(i, m)
+    return lists
+
+
+def rank_program(g, core, T, topo):
+    me = T.rank_of(core)
+    if me is None:
+        return
+    others = [r for r in range(4) if r != me]
+    place = lambda src, dst: [r for r in range(4) if r != dst].index(src)
+
+    def far(r):
+        a, b = topo.chip(core), topo.chip(T.cores[r])
+        return 2 if topo.mates(a, b) else 1 if topo.same_plane(a, b) else 0
+    order = sorted(others, key=far)
+
+    ops, wrote, readers = [], {}, {}
+    total = {}
+    kinds = {"u8": dt.uint8, "u32": dt.uint32}
+
+    def mat(o):
+        p, z = o[7] or (0, SCRATCH[o[1]][1][0])
+        x = T[o[1]][p:z, o[2]:o[3]] if o[4] == 1 else T[o[1]][p:z, o[2]:o[3]:o[4]]
+        if o[5]:
+            x = x.bitcast(kinds[o[5]])
+        return x.indirect(mat(o[6])) if o[6] else x
+
+    def add(q, fn, outs, ins, cost, lat=0.0, sem=None, extra=()):
+        i, deps = len(ops), set(extra)
+        for o in list(ins) + list(outs):
+            if o[6]:
+                ins = list(ins) + [o[6]]
+        for o in ins:
+            if o[1] != "ps":
+                for k in _keys(o):
+                    if k in wrote:
+                        deps.add(wrote[k])
+                    readers.setdefault(k, []).append(i)
+        for o in list(outs) + [o for o in ins if o[1] == "ps"]:
+            for k in _keys(o):
+                if k in wrote:
+                    deps.add(wrote[k])
+                deps.update(readers.pop(k, ()))
+                wrote[k] = i
+        deps.discard(i)
+        ops.append({"q": q, "fn": fn, "deps": deps, "cost": cost, "lat": lat, "sem": sem})
+        return i
+
+    V = g.vector
+    calls = {"copy": V.tensor_copy, "tt": V.tensor_tensor, "ts": V.tensor_scalar, "set": V.memset, "tr": V.transpose,
+             "scan": V.tensor_tensor_scan, "q": V.quantize_mx, "act": g.scalar.activation, "mx": g.tensor.matmul_mx,
+             "iota": lambda *a: g.iota(*a, allow_small_or_imprecise_dtypes=True), "iota32": g.iota, "pb": g.partition_broadcast}
+
+    def do(q, name, args, extra=()):
+        k = 2 if name == "q" else 1
+        fn = lambda: calls[name](*[mat(a) if _isop(a) else a for a in args])
+        return add(q, fn, args[:k], [a for a in args[k:] if _isop(a)], _cost(name.replace("32", ""), args), 0.0, "own", extra)
+
+    v = lambda name, *args, extra=(): do("v", name, args, extra)
+    act = lambda *args: do("s", "act", args)
+    mx = lambda *args: do("t", "mx", args)
+    iota = lambda *args: do("p", "iota", args)
+
+    def dma(q, sem, out, in_, outs, ins, extra=(), lat=2.1):
+        e = {"y": g.sync, "s": g.scalar}[q]
+        total[sem] = total.get(sem, 0) + 16
+        return add(q, lambda: e.dma_start(out(), in_()), outs, ins, 0.06, lat, sem, extra)
+
+    def send(dst, out, in_, sem, *more):
+        c = T.cores[dst]
+        rid, pid, _ = topo.addr(c)
+        total["sent"] = total.get("sent", 0) + len(topo.engines(core, c))
+        return add("p", lambda: g.remote_dma(mat(out), mat(in_), T.sem[sem], T.sem["sent"], pid, rid, topo.mask(core, c)), [], [in_] + list(more), 0.25)
+
+    def arrive(sem, src, writes, outs, lat, extra):
+        total[sem] = total.get(sem, 0) + writes * sum(len(topo.engines(T.cores[s], core)) for s in src)
+        return add(None, None, outs, [], 0.0, lat, sem, extra)
+
+    def pick(to, a, z, win, c, d, off):
+        v("copy", _cast(_o(to, a, z), "u32"), _ind(_cast(_o(win, c, d), "u32"), off))
+        act(_o(to + "s", a, z), _ind(_o(win + "s", c, d), off), F.Copy)
+
+    o, H, W = _o, [(0, 128), (128, 256)], [(0, 64), (64, 128)]
+    f = lambda k: _o("sf", k, k + 1)
+    role = lambda b: _o(b, 3, 256, 4)
+    ps = lambda b, n: _o("ps", 512 * b, 512 * b + n)
+    ones = lambda a, z: _o("cb", 384 + a, 384 + z)
+
+    dma("s", "dr", lambda: T.rtt[:, 0:16], lambda: T.rt[:, 0:16], [o("rtt", 0, 16)], [])
+    dma("y", "dx", lambda: T.xt[:, 64:576], lambda: T.x[:, 0:512], [o("xt", 64, 576)], [], (), 2.6)
+    dx = dma("y", "dx2", lambda: T.xt[:, 576:960], lambda: T.x[:, 512:896], [o("xt", 576, 960)], [], (), 3.0)
+    dma("y", "dw", lambda: T.wt[:, :], lambda: T.w[:, :], [o("wt")], [], (dx,), 4.5)
+    dma("y", "du", lambda: T.ut[:, 0:8], lambda: T.u[:, 0:8], [o("ut", 0, 8)], [], (dx,), 4.8)
+    dma("y", "dv", lambda: T.vt[:, :], lambda: T.v[:, :], [o("vt")], [], (dx,), 5.0)
+
+    do("p", "iota32", (o("si", 0, 1), [[0, 1]], 0, 1))
+    for k in (0, 240):
+        iota(o("tokf", k, k + 240), [[1, 240]], 0, 0)
+    iota(o("kp"), [[0, 15], [256, 4]], 64 - FAR, 0)
+    fill = lambda out: iota(out, [[0, _width(out)]], 0, 0)
+    fill(o("el", 0, 544))
+    fill(o("el", 544, 1088))
+    iota(o("kv"), [[1, 16], [0, 4]], 0, 0)
+    iota(o("ka"), [[0, 16], [-1, 4]], 99, 0)
+    iota(o("kb"), [[0, 16], [2, 4]], 1, 0)
+    for name in ("tabw", "lab2", "qo", "wnw", "m2"):
+        fill(o(name))
+    v("set", o("rtt", 16, 496), 0.0)
+    v("set", o("zero"), 0.0)
+    v("set", o("sl"), 8)
+    v("set", o("ul"), 0)
+    v("set", o("xt", 0, 64), 0.0)
+    v("set", o("xt", 960, 1088), 0.0)
+    v("set", o("rst"), 1.0)
+    v("set", o("rst", 0, 256, 4), 0.0)
+    v("set", ones(0, 256), 1.0)
+    v("ts", o("si", 1, 2), o("si", 0, 1), 15, None, A.bitwise_and)
+    v("ts", o("si", 2, 3), o("si", 0, 1), 15, 2, A.bitwise_and, A.logical_shift_right)
+    v("ts", o("si", 3, 4), o("si", 0, 1), 3, None, A.bitwise_and)
+    v("ts", o("si", 4, 5), o("si", 0, 1), 16, 4, A.bitwise_and, A.logical_shift_right)
+    v("copy", o("sf", 0, 4), o("si", 1, 5))
+    v("ts", f(4), f(2), f(1), None, A.is_lt)
+    v("ts", f(5), f(2), 3.0, None, A.is_lt)
+    v("ts", f(6), f(1), 116.0, None, A.add)
+    v("ts", f(7), f(2), -7.0, None, A.add)
+    v("tt", f(8), f(7), f(4), A.subtract)
+    v("tt", f(9), f(6), f(5), A.mult)
+    v("tt", f(10), f(8), f(5), A.mult)
+    v("ts", o("sl", 0, 9, 2), o("zero", 0, 5), f(10), 8.0, A.add, A.add)
+    v("ts", o("sl", 10, 19, 2), o("zero", 0, 5), f(9), 8.0, A.add, A.add)
+    v("ts", f(13), f(3), -1.0, 1.0, A.mult, A.add)
+    v("ts", f(20), f(3), 16.0, None, A.mult)
+    v("ts", f(15), f(1), 2.0, -16.0, A.is_lt, A.mult)
+    v("tt", f(17), f(15), f(13), A.mult)
+    v("ts", f(11), f(2), 0.0, 8.0, A.is_equal, A.mult)
+    v("ts", f(12), f(2), 3.0, -8.0, A.is_equal, A.mult)
+    v("tt", f(14), f(11), f(12), A.add)
+    v("ts", f(16), f(4), -1e-30, None, A.mult)
+    v("ts", f(18), f(3), 16.0, 31.0 - 64.0, A.mult, A.add)
+    act(o("tok"), o("tokf"), F.Identity, f(20))
+
+    v("ts", o("rtt", 496, 512), o("rtt", 0, 16), -1.0, None, A.mult)
+    v("q", o("rq"), o("rqs"), o("rtt", 0, 512))
+    pick("rr", 0, 144, "rq", 0, 128, o("sl", 0, 9))
+    pick("rr", 144, 288, "rq", 0, 128, o("sl", 10, 19))
+    for h, (x0, x1) in enumerate([(0, 144), (144, 272)]):
+        v("q", o("xq", x0, x1), o("xqs", x0, x1), o("xt", 4 * x0, 4 * x1))
+        for j, (lo, sh) in enumerate([(0, 0), (16, 16), (144, 0), (160, 16)]):
+            sh += 128 * h
+            mx(ps(h, 128), o("rr", lo, lo + 128), o("rrs", lo, lo + 128), o("xq", sh, sh + 128), o("xqs", sh, sh + 128), j == 0, j == 3)
+
+    for h, s in enumerate(H):
+        v("ts", o("a1", *s), ps(h, 128), f(16), f(14), A.is_gt, A.add)
+        v("tr", o("a2", *s), o("a1", *s))
+        v("scan", o("cc", *s), o("rst", *s), o("a2", *s), 0.0, A.mult, A.add)
+        v("ts", o("mm", *s), o("cc", *s), 1.5, None, A.is_lt)
+        v("tr", o("nn", *s), o("mm", *s))
+        v("scan", o("pp", *s), ones(*s), o("nn", *s), o("pp", 127, 128) if h else f(17), A.mult, A.add)
+        v("tr", o("tp", *s), o("pp", *s))
+    for k in range(2):
+        v("ts", o("pe", *W[k]), role("cc"), float(k), float(FAR), A.is_equal, A.mult)
+        v("tt", o("pp2", 60 * k, 60 * k + 60), o("pe", 64 * k, 64 * k + 60), o("kp"), A.add)
+    for x0, x1 in ((0, 32), (32, 60)):
+        for k in (0, 60):
+            v("tt", o("pab", k + x0, k + x1), o("tp", 4 * x0 + 3, 4 * x1, 4), o("pp2", k + x0, k + x1), A.add)
+    v("scan", o("t1"), o("rst", 0, 120), o("pab"), 0.0, A.mult, A.max)
+    v("ts", o("off1"), o("t1", 3, 120, 4), f(18), None, A.add)
+    after = [v("copy", _ind(o("el"), o("off1")), o("tok"))]
+
+    def wrap(x, lo, n):
+        xn, xp, wl, off = "xn" + x, "xp" + x, "wl" + x, "off2" + ("a" if x else "")
+        v("ts", o(xn), o("lt", lo, lo + 16 * n, 16), f(13), None, A.mult)
+        v("ts", o(xp), o("lt", lo, lo + 16 * n, 16), f(3), None, A.mult)
+        v("tt", o(wl, 0, n, 2), o(xn, 0, n, 2), o(xp, 1, n, 2), A.add)
+        v("tt", o(wl, 1, n - 1, 2), o(xn, 3, n, 2), o(xp, 0, n - 2, 2), A.add)
+        return v("copy", o(off, 0, n - 1), o(wl, 0, n - 1))
+
+    sent = []
+
+    def token(e, off):
+        pick("xs", 128 * e, 128 * e + 128, "xq", 0, 272, off)
+        if e != me:
+            i = place(me, e)
+            sent.append(send(e, _cast(o("xl", 128 * i, 128 * i + 128), "u8"), _cast(o("xs", 128 * e, 128 * e + 128), "u8"), "xa%d" % i))
+            sent.append(send(e, o("xls", 128 * i, 128 * i + 128), o("xss", 128 * e, 128 * e + 128), "xa%d" % i, o("xs", 128 * e, 128 * e + 128)))
+    for n, e in enumerate(order + [me]):
+        v("tr", o("lt", 160 * e, 160 * e + 160), o("el", 256 * e + 32, 256 * e + 192))
+        if n == 0:
+            after = [wrap("1", 160 * e, 10)]
+            token(e, o("off2a", 0, 8))
+    wrap("", 0, 40)
+    for e in order[1:] + [me]:
+        token(e, o("off2", 10 * e, 10 * e + 8))
+
+    v("set", o("hb", 512, 576), 0.0, extra=after)
+    v("set", o("ut", 8, 512), 0.0, extra=after)
+    for i in range(4):
+        v("q", o("wq", 128 * i, 128 * i + 128), o("wqs", 128 * i, 128 * i + 128), o("wt", 512 * i, 512 * i + 512), extra=after)
+    v("q", o("uq"), o("uqs"), o("ut"), extra=after)
+    pick("ur", 0, 128, "uq", 0, 128, o("ul"))
+
+    def chunk(xc, lo, hlo, hn, hc, hto, banks):
+        for i, b in enumerate(banks):
+            mx(ps(b, 128), o("wq", 128 * i, 128 * i + 128), o("wqs", 128 * i, 128 * i + 128), o(xc, lo, lo + 128), o(xc + "s", lo, lo + 128), True, True)
+            out = o("hb", hlo + i, hlo + 512, 4)
+            if i % 2 == 0:
+                act(out, ps(b, 128), F.Relu, 0.0, 0.0625)
+            else:
+                v("ts", out, ps(b, 128), 0.0, 0.0625, A.max, A.mult)
+        v("q", o(hc, hto, hto + hn), o(hc + "s", hto, hto + hn), o("hb", hlo, hlo + 4 * hn))
+
+    chunk("xs", 128 * me, 0, 144, "zq", 0, (0, 1, 2, 3))
+    fills = []
+    for t in ("gt", "gtt"):
+        fills.append(act(o(t, 0, 480), o("tokf"), F.Identity, -9e29, 0.0))
+        fills.append(act(o(t, 480, 520), o("tokf", 0, 40), F.Identity, -9e29, 0.0))
+        act(o(t, 520, 528), o("tokf", 0, 8), F.Identity, 9e29, 0.0)
+    mx(ps(0, 128), o("ur"), o("urs"), o("zq", 0, 128), o("zqs", 0, 128), True, True)
+    act(o("gt", 0, 128), ps(0, 128), F.Copy)
+    act(o("gtt", 0, 128), ps(0, 128), F.Copy)
+
+    rel = [0 if e == me else 128 + 128 * others.index(e) for e in range(4)]
+    for e in range(4):
+        act(o("kr", e, 64, 4), o("zero"), F.Identity, float(rel[e] - 1 - 512))
+    v("ts", o("mab", 0, 64), role("cc"), 0.0, None, A.is_equal, extra=after)
+    v("ts", o("mab", 64, 128), role("cc"), 1.0, None, A.is_equal, extra=after)
+    v("ts", o("tk"), role("tp"), 128.5, None, A.is_lt, extra=after)
+    v("tt", o("v2"), role("tp"), o("kr"), A.add, extra=after)
+    v("tt", o("abe", 0, 64), o("mab", 0, 64), o("tk"), A.mult, extra=after)
+    v("tt", o("abe", 64, 128), o("mab", 64, 128), o("tk"), A.mult, extra=after)
+    v("tt", o("pab2", 0, 64), o("abe", 0, 64), o("v2"), A.mult)
+    v("tt", o("pab2", 64, 128), o("abe", 64, 128), o("v2"), A.mult)
+    v("scan", o("t2"), o("rst", 0, 128), o("pab2"), 0.0, A.mult, A.add)
+    v("ts", o("off3"), o("t2", 3, 128, 4), 512.0, None, A.add)
+    v("ts", o("kv2"), o("kv"), f(13), None, A.subtract, extra=after)
+    v("ts", o("kv"), o("kv2"), 0.0, None, A.is_ge, extra=after)
+    v("ts", o("kv3"), o("kv2"), 13.5, None, A.is_lt, extra=after)
+    v("tt", o("kv2"), o("kv"), o("kv3"), A.mult)
+    v("tt", o("ae"), o("abe", 0, 64), o("kv2"), A.mult)
+    v("tt", o("be"), o("abe", 64, 128), o("kv2"), A.mult)
+    v("tt", o("de"), o("ae"), o("be"), A.subtract)
+    v("set", o("wa", 240, 256), 0.0, extra=after)
+    for k in range(3):
+        v("ts", f(25 + k), f(0), float(16 * k), 2.0, A.add, A.mult, extra=after)
+        v("ts", f(28 + k), f(25 + k), 2.0, None, A.add, extra=after)
+        v("ts", o("bt", 65 * k, 588, 196), o("zero", 0, 3), f(28 + k), -64.0, A.add, A.mult, extra=after)
+    v("set", o("rsl"), 1.0, extra=after)
+    v("set", o("rsl", 0, 196, 65), 0.0, extra=after)
+
+    asked = []
+    BANKS = [(4, 5, 6, 7), (0, 1, 2, 3), (4, 5, 6, 3)]
+    for n, s in enumerate(order):
+        i = others.index(s)
+        arrive("xa%d" % i, [s], 2, [o("xl", 128 * i, 128 * i + 128), o("xls", 128 * i, 128 * i + 128)], 2.4, sent[2 * n:2 * n + 2])
+        chunk("xl", 128 * i, 576 + 512 * i, 128, "hq", 128 * i, BANKS[n])
+        b = BANKS[n][0 if n else 3]
+        mx(ps(b, 128), o("hq", 128 * i, 128 * i + 128), o("hqs", 128 * i, 128 * i + 128), o("uq"), o("uqs"), True, True)
+        act(o("qs", i, i + 1), ps(b, 1), F.Copy)
+        k, c = place(me, s), T.cores[s]
+        rid, pid, _ = topo.addr(c)
+        total["sent"] += len(topo.engines(core, c))
+        asked.append(add("p", lambda i=i, k=k, c=c, rid=rid, pid=pid: g.remote_dma(T.dg[128 * k:128 * k + 128, :], T.qs[:, i:i + 1], T.sem.qa, T.sem.sent, pid, rid, topo.mask(core, c)),
+                         [], [o("qs", i, i + 1)], 0.25))
+
+    v("set", o("tab", 256, 288), 0.0, extra=after)
+    v("set", o("tab", 544, 576), 0.0, extra=after)
+    for e in range(4):
+        v("set", _part(f(24), 32 * e), float(rel[e] - 520), extra=after)
+        v("copy", _part(o("offl", 16, 24), 32 * e), _part(o("off2", 10 * e, 10 * e + 8), 32 * e))
+    act(o("own"), o("tokf", 0, 128), F.Identity, f(24))
+    for k in range(2):
+        v("ts", o("tabw", 256 * k, 256 * k + 256, 16), o("t2", 64 * k + 3, 64 * k + 64, 4), 256.0, None, A.add)
+        v("tr", o("tab", 288 * k, 288 * k + 256), o("tabw", 256 * k, 256 * k + 256))
+        act(o("gab2", 128 * k, 128 * k + 128), _ind(o("tab", 288 * k, 288 * k + 272), o("offl", 16, 24)), F.Identity, -264.0)
+    for k, how in enumerate((A.is_equal, A.not_equal)):
+        s = H[k]
+        v("tt", o("isa", *s), o("gab2", 0, 128), o("own"), how, extra=asked)
+        v("tt", o("lab", *s), o("isa", *s), o("gab2", *H[1 - k]), A.mult)
+        act(o("lab2", 160 * k + 16, 160 * k + 144), o("lab", *s), F.Copy)
+        v("tr", o("lt1", *s), o("lab", *s))
+        v("tr", o("lt0", *s), o("lab2", 160 * k + 32, 160 * k + 160))
+        v("ts", o("offl", 8 * k, 8 * k + 8, 2), o("lt1", s[0], s[1], 32), 520.0, None, A.add)
+        v("ts", o("offl", 8 * k + 1, 8 * k + 8, 2), o("lt0", s[0], s[1], 32), 520.0, None, A.add)
+
+    arrive("qa", others, 1, [o("dg")], 1.7, asked)
+    late = []
+    for n, e in enumerate(order):
+        i, q = others.index(e), "ys"
+        late.append(dma(q[n % 2], "dgt", lambda e=e: T.gt[32 * e:32 * e + 1, 128:512], lambda: T.dg[:, :], [_part(o("gt", 128, 512), 32 * e)], [o("dg")]))
+        late.append(dma(q[1 - n % 2], "dgt", lambda e=e: T.qo[32 * e:32 * e + 1, :], lambda i=i: T.dg[128 * i:128 * i + 128, :],
+                        [_part(o("qo"), 32 * e)], [o("dg")]))
+    for k in range(8):
+        dma("ys"[k % 2], "dgo", lambda k=k: T.gtt[16 * k:16 * k + 1, 128:512], lambda: T.dg[:, :],
+            [o("gtt", 128 + 48 * k, 176 + 48 * k)], [o("dg")], fills)
+    v("tt", o("a1", 0, 128), _ind(o("gt"), o("offl", 0, 8)), o("qo"), A.is_le)
+    v("tt", o("a1", 128, 256), _ind(o("gt"), o("offl", 8, 16)), o("qo"), A.is_lt)
+    counted = v("scan", o("a2", 0, 128), o("a1", 0, 128), o("a1", 128, 256), 0.0, A.add, A.add)
+    told = []
+    v("tt", o("vp"), o("a2", 0, 128, 2), o("a2", 1, 128, 2), A.add)
+    for n, e in enumerate(order):
+        s, t = (64 * n, 64 * n + 64), 196 * n
+        do("p", "pb", (o("cb", *s), _part(o("vp"), 32 * e, 1), 128))
+        for k in range(3):
+            v("ts", o("bt", t + 65 * k + 1, t + 65 * k + 65), o("cb", *s), f(25 + k), f(28 + k), A.max, A.min)
+        v("scan", o("sc", t, t + 195), o("rsl", 0, 195), o("bt", t, t + 195), 0.0, A.mult, A.subtract)
+        v("ts", o("ls", 4 * e, 4 * e + 3), o("sc", t + 64, t + 195, 65), 127.0, None, A.min)
+        i = place(me, e)
+        told.append(send(e, o("la", 4 * i, 4 * i + 3), o("ls", 4 * e, 4 * e + 3), "ar%d" % i))
+
+    act(o("gab", 0, 128), _ind(o("gtt"), o("off3", 16, 24)), F.Copy)
+    v("copy", o("gab", 128, 240), _ind(o("gtt"), o("off3", 24, 31)), extra=(counted,))
+    v("tt", o("wa", 0, 128), _ind(o("gtt"), o("off3", 0, 8)), o("gab", 0, 128), A.is_ge, extra=(counted,))
+    v("tt", o("wa", 128, 240), _ind(o("gtt"), o("off3", 8, 15)), o("gab", 128, 240), A.is_ge)
+    quarter = lambda t, h: o(t, 3 + 128 * h, 128 + 128 * h, 4)
+    for s in H:
+        v("tr", o("wat", *s), o("wa", *s))
+    for e in range(4):
+        v("tt", o("x4", e, 64, 4), o("wat", 0, 256, 16), o("de", e, 64, 4), A.mult)
+    for h, s in enumerate(H):
+        v("tt", quarter("m2", h), o("x4", 32 * h, 32 * h + 32), o("be", 32 * h, 32 * h + 32), A.add)
+        v("tr", o("n2", *s), o("m2", *s))
+        v("scan", o("rc", *s), ones(*s), o("n2", *s), o("rc", 127, 128) if h else 0.0, A.mult, A.add)
+        v("tr", o("rtr", *s), o("rc", *s))
+
+    for e in range(4):
+        act(o("kz", e, 64, 4), o("zero"), F.Identity, float(-1 - 128 if e == me else 144 + 48 * others.index(e) - 1 - 128))
+    v("q", o("vq"), o("vqs"), o("vt"))
+    v("ts", o("h1"), role("rtr"), 48.5, None, A.is_lt)
+    v("copy", o("xz"), role("rtr"))
+    v("copy", o("xz", me, 64, 4), o("tp", 4 * me + 3, 256, 16))
+    v("tt", o("hm"), role("m2"), o("h1"), A.mult)
+    v("tt", o("z1"), o("xz"), o("kz"), A.add)
+    v("tt", o("z2"), o("z1"), o("hm"), A.mult)
+    v("scan", o("z3"), o("rst", 0, 64), o("z2"), 0.0, A.mult, A.add)
+    v("ts", o("zn"), o("z3", 3, 64, 4), f(13), None, A.mult)
+    v("ts", o("zp"), o("z3", 3, 64, 4), f(3), None, A.mult)
+    v("tt", o("zl"), o("zn", 1, 15), o("zp", 0, 14), A.add)
+    v("ts", o("off5"), o("zl"), 128.0, None, A.add)
+    v("tt", o("w1"), role("m2"), o("ka"), A.mult)
+    v("tt", o("w2"), o("hm"), o("kb"), A.mult)
+    v("tt", o("w3"), o("w2"), o("w1"), A.add)
+    v("scan", o("w4"), o("rst", 0, 64), o("w3"), 0.0, A.mult, A.add)
+    v("ts", o("wnw", 0, 256, 16), o("w4", 3, 64, 4), -100.0, None, A.add)
+    v("tr", o("wnf"), o("wnw"))
+    dma("y", "out", lambda: T.wn[:, :], lambda: T.wnf[16:17, 0:224], [], [o("wnf")])
+
+    came = []
+    for n, s in enumerate(order):
+        i = others.index(s)
+        arrive("ar%d" % i, [s], 1, [o("la", 4 * i, 4 * i + 3)], 1.7, told[n:n + 1])
+        pick("hs", 48 * i, 48 * i + 48, "hq", 128 * i, 128 * i + 128, o("la", 4 * i, 4 * i + 3))
+        k = 144 + 48 * place(me, s)
+        came.append(send(s, _cast(o("zq", k, k + 48), "u8"), _cast(o("hs", 48 * i, 48 * i + 48), "u8"), "ha"))
+        came.append(send(s, o("zqs", k, k + 48), o("hss", 48 * i, 48 * i + 48), "ha", o("hs", 48 * i, 48 * i + 48)))
+
+    arrive("ha", others, 2, [o("zq", 144, 288), o("zqs", 144, 288)], 2.0, came)
+    pick("z", 0, 128, "zq", 0, 288, o("off5", 0, 8))
+    pick("z", 128, 224, "zq", 0, 288, o("off5", 8, 14))
+    mx(ps(0, 128), o("vq"), o("vqs"), o("z", 0, 128), o("zs", 0, 128), True, True)
+    mx(ps(1, 128), o("vq"), o("vqs"), o("z", 96, 224), o("zs", 96, 224), True, True)
+    v("copy", o("ysb", 0, 128), ps(0, 128))
+    v("copy", o("ysb", 128, 224), o("ps", 544, 640))
+    dma("y", "out", lambda: T.oc[:, :], lambda: T.z[:, 0:224].bitcast(dt.uint8), [], [o("z")])
+    for k in range(4):
+        dma("s" if k % 2 == 0 else "y", "out", lambda k=k: T.osc[4 * k:4 * k + 4, :], lambda k=k: T.zs[32 * k:32 * k + 4, :], [], [o("zs")])
+    for a, z in ((0, 128), (128, 224)):
+        dma("y", "out", lambda a=a, z=z: T.y[:, a:z], lambda a=a, z=z: T.ysb[:, a:z], [], [o("ysb", a, z)])
+
+    queue = {"v": V, "s": g.scalar, "t": g.tensor, "p": g, "y": g.sync}
+    lists = _order(ops)
+    mark = {}
+    for q, items in lists.items():
+        n = 0
+        for i in items:
+            if ops[i]["sem"] == "own":
+                n += 1
+                mark[i] = (q, n)
+        total[q] = n
+    for i, x in enumerate(ops):
+        if x["sem"] and x["sem"] != "own":
+            mark[i] = (x["sem"], total[x["sem"]])
+    seen = {}
+    for q, items in lists.items():
+        for i in items:
+            best = {}
+            for d in ops[i]["deps"]:
+                if d in mark and not (q == "t" and ops[d]["q"] == "t"):
+                    s, n = mark[d]
+                    best[s] = max(n, best.get(s, 0))
+            for s, n in sorted(best.items()):
+                if seen.get((q, s), 0) < n:
+                    queue[q].wait_ge(T.sem[s], n)
+                    seen[(q, s)] = n
+            call = ops[i]["fn"]()
+            if ops[i]["sem"]:
+                call.then_inc(T.sem[mark[i][0]], 1 if ops[i]["sem"] == "own" else 16)
+    for s, n in sorted(total.items()):
+        if n and seen.get(("p", s), 0) < n:
+            g.wait_ge(T.sem[s], n)

@@ -2,24 +2,21 @@ from concourse.mybir import dt, AluOpType as A, ActivationFunctionType as F
 
 
 def _buffers():
-    d = {"dg": ("dram", [384, 1], "float32"), "ps": ("psum", [128, 4096], "float32")}
+    d = {"ps": ("psum", [128, 4096], "float32")}
     kinds = {
-        "bfloat16": "xt 1088 rtt 512 wt 2048 ut 512 vt 512 hb 2112 rst 256 one 256 tok 480 a1 256 a2 256 cc 256 mm 256 nn 256 "
-                    "pp 256 tp 256 el 1088 lt 640 wa 256 wat 256 m2 256 n2 256 rc 256 rtr 256 "
-                    "tabw 512 tab 576 vp 64 bt 588 sc 588 rsl 196",
-        "float32": "ysb 224 sf 40 zero 16 tokf 480 kp 60 pe 128 pp2 128 ka 64 kb 64 kz 64 kr 64 kv 64 kv2 64 kv3 64 mab 128 pab 120 "
-                   "t1 120 xn 40 xp 40 wl 40 xn1 10 xp1 10 wl1 10 tk 64 abe 128 v2 64 pab2 128 t2 128 ae 64 be 64 de 64 qs 4 "
-                   "gt 528 gtt 528 gab 256 x4 64 qo 128 own 128 gab2 256 isa 256 lab 256 lab2 320 lt1 256 lt0 256 h1 64 hm 64 xz 64 "
-                   "z1 64 z2 64 z3 64 zn 16 zp 16 zl 14 w1 64 w2 64 w3 64 w4 64 wnw 256 wnf 256",
-        "uint16": "sl 20 ul 8 off1 30 off2 40 off2a 10 off3 32 offl 24 off5 14 ls 16 la 12",
-        "int32": "si 8",
+        "bfloat16": "xt 1024 rtt 512 wt 2048 ut 512 vt 512 hb 2112 d0 896 d1 896 uu 896 bt 912 sc 912 rsl 912 "
+                    "i3 672 i16 256 rst3 672 rst16 256 mask 256 one 224 sg 672 wsc 688 nn 224 pp 224 zr 240 gz 512 gs 512 "
+                    "wg 128 ws 128 a1 256 a2 128 a3 128 bt2 384 sc2 384 rs2 384 cn 240 zm 224 zs2 224 g2 224 g3 224",
+        "float32": "ysb 224 sf 32 zero 32 kl0 8 klo 8 khi 8 ga 32 gb 32 gc 32 gd 32 gx 32 gy 24 gp 16 gm 16 gl 16 "
+                   "qs 192 ql 12 rep 192 gt 528 qo 128 won 14 h1 14 hm 14 xz 14 w1 14 w2 14 zw 28 t1 28 s1 28 t2 28 s2 28 wnw 32 wnf 32",
+        "uint16": "sl 20 ul 8 off2 32 ol3 8 offl 16 offp 14 off5 14 ls 16 la 12",
+        "int32": "si 4 sj 32",
     }
     for t, text in kinds.items():
         w = text.split()
         for name, n in zip(w[::2], w[1::2]):
             d[name] = ("sbuf", [128, int(n)], t)
-    d["cb"] = d.pop("one")[:1] + ([128, 640], "bfloat16")
-    w = "xq 272 rq 128 rr 288 wq 512 uq 128 ur 128 vq 128 xs 512 xl 384 hq 384 hs 144 zq 288 z 224".split()
+    w = "xq 256 rq 128 rr 320 wq 512 uq 128 ur 128 vq 128 xs 512 xl 384 hq 384 hs 144 zq 288 z 224".split()
     for name, n in zip(w[::2], w[1::2]):
         d[name] = ("sbuf", [128, int(n)], "float8_e4m3fn_x4")
         d[name + "s"] = ("sbuf", [128, int(n)], "uint8")
@@ -27,9 +24,9 @@ def _buffers():
 
 
 SCRATCH = _buffers()
-SEMAPHORES = ["v", "s", "t", "p", "dx", "dx2", "dr", "dw", "du", "dv", "dgt", "dgo", "out", "sent", "qa", "ha"] \
-    + ["xa%d" % i for i in range(3)] + ["ar%d" % i for i in range(3)]
-FAR = 4096
+SEMAPHORES = ["v", "s", "t", "p", "dx", "dx2", "dr", "dw", "du", "dv", "out", "sent", "ha"] \
+    + ["xa%d" % i for i in range(3)] + ["qa%d" % i for i in range(3)] + ["ar%d" % i for i in range(3)]
+BIG = 2.0 ** 27
 WAKE, CYC = 0.12, 0.00083
 
 
@@ -71,14 +68,10 @@ def _cost(name, args):
     if name == "q":
         return .012 + .00088 * n
     ops = [a for a in args if _isop(a)]
-    if name == "pb":
-        return .14 + 4 * n * CYC
     if name == "iota":
         return .13 + 2 * n * CYC
     if name == "act":
         return .065 + n * CYC * (1.5 if args[1][6] else 1)
-    if out[6]:
-        return .05 + 3 * n * CYC
     if any(a[6] for a in ops):
         return .05 + 1.6 * n * CYC
     two = all(SCRATCH[a[1]][2] in ("bfloat16", "uint16") for a in ops if _width(a) > 1)
@@ -189,7 +182,7 @@ def rank_program(g, core, T, topo):
     V = g.vector
     calls = {"copy": V.tensor_copy, "tt": V.tensor_tensor, "ts": V.tensor_scalar, "set": V.memset, "tr": V.transpose,
              "scan": V.tensor_tensor_scan, "q": V.quantize_mx, "act": g.scalar.activation, "mx": g.tensor.matmul_mx,
-             "iota": lambda *a: g.iota(*a, allow_small_or_imprecise_dtypes=True), "iota32": g.iota, "pb": g.partition_broadcast}
+             "iota": lambda *a: g.iota(*a, allow_small_or_imprecise_dtypes=True), "iota32": g.iota}
 
     def do(q, name, args, extra=()):
         k = 2 if name == "q" else 1
@@ -197,7 +190,7 @@ def rank_program(g, core, T, topo):
         return add(q, fn, args[:k], [a for a in args[k:] if _isop(a)], _cost(name.replace("32", ""), args), 0.0, "own", extra)
 
     v = lambda name, *args, extra=(): do("v", name, args, extra)
-    act = lambda *args: do("s", "act", args)
+    act = lambda *args, extra=(): do("s", "act", args, extra)
     mx = lambda *args: do("t", "mx", args)
     iota = lambda *args: do("p", "iota", args)
 
@@ -217,272 +210,223 @@ def rank_program(g, core, T, topo):
         return add(None, None, outs, [], 0.0, lat, sem, extra)
 
     def pick(to, a, z, win, c, d, off):
-        v("copy", _cast(_o(to, a, z), "u32"), _ind(_cast(_o(win, c, d), "u32"), off))
         act(_o(to + "s", a, z), _ind(_o(win + "s", c, d), off), F.Copy)
+        return v("copy", _cast(_o(to, a, z), "u32"), _ind(_cast(_o(win, c, d), "u32"), off))
 
-    o, H, W = _o, [(0, 128), (128, 256)], [(0, 64), (64, 128)]
+    o = _o
     f = lambda k: _o("sf", k, k + 1)
-    role = lambda b: _o(b, 3, 256, 4)
-    ps = lambda b, n: _o("ps", 512 * b, 512 * b + n)
-    ones = lambda a, z: _o("cb", 384 + a, 384 + z)
+    ps = lambda b, n, a=0: _o("ps", 512 * b + a, 512 * b + a + n)
+    blk = lambda x, e: _part(x, 32 * e)
+    half = lambda x, h: _part(x, 64 * h, 64)
+
+    def move(n, out, in_, extra=()):
+        return v("copy", out, in_, extra=extra) if n % 2 == 0 else act(out, in_, F.Copy, extra=extra)
 
     dma("s", "dr", lambda: T.rtt[:, 0:16], lambda: T.rt[:, 0:16], [o("rtt", 0, 16)], [])
-    dma("y", "dx", lambda: T.xt[:, 64:576], lambda: T.x[:, 0:512], [o("xt", 64, 576)], [], (), 2.6)
-    dx = dma("y", "dx2", lambda: T.xt[:, 576:960], lambda: T.x[:, 512:896], [o("xt", 576, 960)], [], (), 3.0)
-    dma("y", "dw", lambda: T.wt[:, :], lambda: T.w[:, :], [o("wt")], [], (dx,), 4.5)
-    dma("y", "du", lambda: T.ut[:, 0:8], lambda: T.u[:, 0:8], [o("ut", 0, 8)], [], (dx,), 4.8)
-    dma("y", "dv", lambda: T.vt[:, :], lambda: T.v[:, :], [o("vt")], [], (dx,), 5.0)
+    dma("y", "dx", lambda: T.xt[:, 0:512], lambda: T.x[:, 0:512], [o("xt", 0, 512)], [], (), 2.6)
+    dx = dma("y", "dx2", lambda: T.xt[:, 512:896], lambda: T.x[:, 512:896], [o("xt", 512, 896)], [], (), 3.0)
+    dma("y", "dw", lambda: T.wt[:, :], lambda: T.w[:, :], [o("wt")], [], (dx,), 4.0)
+    dma("y", "du", lambda: T.ut[:, :], lambda: T.u[:, :], [o("ut")], [], (dx,), 4.3)
+    dma("y", "dv", lambda: T.vt[:, :], lambda: T.v[:, :], [o("vt")], [], (dx,), 4.6)
 
     do("p", "iota32", (o("si", 0, 1), [[0, 1]], 0, 1))
-    for k in (0, 240):
-        iota(o("tokf", k, k + 240), [[1, 240]], 0, 0)
-    iota(o("kp"), [[0, 15], [256, 4]], 64 - FAR, 0)
-    fill = lambda out: iota(out, [[0, _width(out)]], 0, 0)
-    fill(o("el", 0, 544))
-    fill(o("el", 544, 1088))
-    iota(o("kv"), [[1, 16], [0, 4]], 0, 0)
-    iota(o("ka"), [[0, 16], [-1, 4]], 99, 0)
-    iota(o("kb"), [[0, 16], [2, 4]], 1, 0)
-    for name in ("tabw", "lab2", "qo", "wnw", "m2"):
-        fill(o(name))
+    do("p", "iota32", (o("sj", 0, 8), [[1, 4], [0, 2]], 124, 0))
+    do("p", "iota32", (o("sj", 20, 32), [[1, 6], [0, 2]], 1, 0))
+    iota(o("kl0"), [[256, 8]], 0, 0)
+    iota(o("i16"), [[0, 16], [1, 16]], 0, 0)
+    iota(o("i3"), [[0, 224], [1, 3]], 0, 0)
+    iota(o("cn"), [[0, 240]], 0, 0)
     v("set", o("rtt", 16, 496), 0.0)
-    v("set", o("zero"), 0.0)
-    v("set", o("sl"), 8)
-    v("set", o("ul"), 0)
-    v("set", o("xt", 0, 64), 0.0)
-    v("set", o("xt", 960, 1088), 0.0)
-    v("set", o("rst"), 1.0)
-    v("set", o("rst", 0, 256, 4), 0.0)
-    v("set", ones(0, 256), 1.0)
+    v("set", o("xt", 896, 1024), 0.0)
+    v("ts", o("sj", 8, 20), o("sj", 20, 32), 3, None, A.bitwise_and)
+    v("copy", o("sl"), o("sj", 0, 20))
     v("ts", o("si", 1, 2), o("si", 0, 1), 15, None, A.bitwise_and)
-    v("ts", o("si", 2, 3), o("si", 0, 1), 15, 2, A.bitwise_and, A.logical_shift_right)
-    v("ts", o("si", 3, 4), o("si", 0, 1), 3, None, A.bitwise_and)
-    v("ts", o("si", 4, 5), o("si", 0, 1), 16, 4, A.bitwise_and, A.logical_shift_right)
-    v("copy", o("sf", 0, 4), o("si", 1, 5))
-    v("ts", f(4), f(2), f(1), None, A.is_lt)
-    v("ts", f(5), f(2), 3.0, None, A.is_lt)
-    v("ts", f(6), f(1), 116.0, None, A.add)
-    v("ts", f(7), f(2), -7.0, None, A.add)
-    v("tt", f(8), f(7), f(4), A.subtract)
-    v("tt", f(9), f(6), f(5), A.mult)
-    v("tt", f(10), f(8), f(5), A.mult)
-    v("ts", o("sl", 0, 9, 2), o("zero", 0, 5), f(10), 8.0, A.add, A.add)
-    v("ts", o("sl", 10, 19, 2), o("zero", 0, 5), f(9), 8.0, A.add, A.add)
-    v("ts", f(13), f(3), -1.0, 1.0, A.mult, A.add)
-    v("ts", f(20), f(3), 16.0, None, A.mult)
-    v("ts", f(15), f(1), 2.0, -16.0, A.is_lt, A.mult)
-    v("tt", f(17), f(15), f(13), A.mult)
-    v("ts", f(11), f(2), 0.0, 8.0, A.is_equal, A.mult)
-    v("ts", f(12), f(2), 3.0, -8.0, A.is_equal, A.mult)
-    v("tt", f(14), f(11), f(12), A.add)
-    v("ts", f(16), f(4), -1e-30, None, A.mult)
-    v("ts", f(18), f(3), 16.0, 31.0 - 64.0, A.mult, A.add)
-    act(o("tok"), o("tokf"), F.Identity, f(20))
+    v("ts", o("si", 2, 3), o("si", 0, 1), 5, None, A.logical_shift_right)
+    v("copy", o("sf", 0, 2), o("si", 1, 3))
+    for i in (1, 2, 3):
+        v("ts", f(1 + i), f(1), 3.5 - i, -1e-30, A.is_gt, A.mult)
+    v("ts", o("sf", 5, 8), o("sf", 2, 5), 2.0, 1e-30, A.mult, A.add)
+    v("ts", f(8), f(0), 16.0, None, A.mult)
+    v("ts", o("klo"), o("kl0"), f(8), None, A.add)
+    v("ts", o("khi"), o("kl0"), f(8), 16.0, A.add, A.add)
+    v("ts", o("bt", 0, 912, 114), o("khi"), -128.0, None, A.mult)
+    v("ts", o("bt", 1, 912, 114), o("khi"), 16.0, None, A.mult)
+    v("set", o("rsl"), 1.0)
+    v("set", o("rsl", 0, 912, 114), 0.0)
+    for k, x in ((0, 4.0), (1, -BIG), (3, 3.5), (4, -BIG), (5, 0.0), (7, BIG / 2)):
+        v("set", o("d0", k, 896, 8), x)
+    for k, x in ((0, BIG), (3, BIG), (4, 0.0), (7, -BIG / 2)):
+        v("set", o("d1", k, 896, 8), x)
+    act(o("rst3"), o("i3"), F.Sign)
+    act(o("rst16"), o("i16"), F.Sign)
+    act(o("one"), o("i16", 0, 224), F.Identity, 1.0, 0.0)
+    act(o("rs2"), o("i3", 0, 384), F.Identity, 1.0, 0.0)
+    act(o("zero"), o("i16", 0, 32), F.Identity, 0.0, 0.0)
+    act(o("wnw"), o("i16", 0, 32), F.Identity, 0.0, 0.0)
+    act(o("zr", 224, 240), o("i16", 0, 16), F.Identity, 0.0, 0.0)
+    act(o("wsc", 672, 688), o("i16", 0, 16), F.Identity, 0.0, 0.0)
+    act(o("hb", 512, 576), o("i16", 0, 64), F.Identity, 0.0, 0.0)
+    act(o("gt", 512, 520), o("i16", 0, 8), F.Identity, -9e29, 0.0)
+    act(o("gt", 520, 528), o("i16", 0, 8), F.Identity, 9e29, 0.0)
 
     v("ts", o("rtt", 496, 512), o("rtt", 0, 16), -1.0, None, A.mult)
     v("q", o("rq"), o("rqs"), o("rtt", 0, 512))
-    pick("rr", 0, 144, "rq", 0, 128, o("sl", 0, 9))
-    pick("rr", 144, 288, "rq", 0, 128, o("sl", 10, 19))
-    for h, (x0, x1) in enumerate([(0, 144), (144, 272)]):
-        v("q", o("xq", x0, x1), o("xqs", x0, x1), o("xt", 4 * x0, 4 * x1))
-        for j, (lo, sh) in enumerate([(0, 0), (16, 16), (144, 0), (160, 16)]):
-            sh += 128 * h
-            mx(ps(h, 128), o("rr", lo, lo + 128), o("rrs", lo, lo + 128), o("xq", sh, sh + 128), o("xqs", sh, sh + 128), j == 0, j == 3)
-
-    for h, s in enumerate(H):
-        v("ts", o("a1", *s), ps(h, 128), f(16), f(14), A.is_gt, A.add)
-        v("tr", o("a2", *s), o("a1", *s))
-        v("scan", o("cc", *s), o("rst", *s), o("a2", *s), 0.0, A.mult, A.add)
-        v("ts", o("mm", *s), o("cc", *s), 1.5, None, A.is_lt)
-        v("tr", o("nn", *s), o("mm", *s))
-        v("scan", o("pp", *s), ones(*s), o("nn", *s), o("pp", 127, 128) if h else f(17), A.mult, A.add)
-        v("tr", o("tp", *s), o("pp", *s))
-    for k in range(2):
-        v("ts", o("pe", *W[k]), role("cc"), float(k), float(FAR), A.is_equal, A.mult)
-        v("tt", o("pp2", 60 * k, 60 * k + 60), o("pe", 64 * k, 64 * k + 60), o("kp"), A.add)
-    for x0, x1 in ((0, 32), (32, 60)):
-        for k in (0, 60):
-            v("tt", o("pab", k + x0, k + x1), o("tp", 4 * x0 + 3, 4 * x1, 4), o("pp2", k + x0, k + x1), A.add)
-    v("scan", o("t1"), o("rst", 0, 120), o("pab"), 0.0, A.mult, A.max)
-    v("ts", o("off1"), o("t1", 3, 120, 4), f(18), None, A.add)
-    after = [v("copy", _ind(o("el"), o("off1")), o("tok"))]
-
-    def wrap(x, lo, n):
-        xn, xp, wl, off = "xn" + x, "xp" + x, "wl" + x, "off2" + ("a" if x else "")
-        v("ts", o(xn), o("lt", lo, lo + 16 * n, 16), f(13), None, A.mult)
-        v("ts", o(xp), o("lt", lo, lo + 16 * n, 16), f(3), None, A.mult)
-        v("tt", o(wl, 0, n, 2), o(xn, 0, n, 2), o(xp, 1, n, 2), A.add)
-        v("tt", o(wl, 1, n - 1, 2), o(xn, 3, n, 2), o(xp, 0, n - 2, 2), A.add)
-        return v("copy", o(off, 0, n - 1), o(wl, 0, n - 1))
+    pick("rr", 0, 128, "rq", 0, 128, o("sl", 0, 8))
+    pick("rr", 128, 256, "rq", 0, 128, o("sl", 8, 16))
+    pick("rr", 256, 320, "rq", 0, 128, o("sl", 16, 20))
+    spot = [("d1", 1), ("d0", 2), ("d1", 2)]
+    for h, n in enumerate((128, 96)):
+        x0 = 128 * h
+        v("q", o("xq", x0, x0 + 128), o("xqs", x0, x0 + 128), o("xt", 4 * x0, 4 * x0 + 512))
+        for first in (True, False):
+            for i in range(3):
+                lo = 0 if first else 128 + 32 * i
+                mx(ps(3 * h + i, 128), o("rr", lo, lo + 128), o("rrs", lo, lo + 128), o("xq", x0, x0 + 128), o("xqs", x0, x0 + 128), first, not first)
+        for i, (name, k) in enumerate(spot):
+            v("ts", o(name, 4 * x0 + k, 4 * (x0 + n), 4), ps(3 * h + i, n), f(2 + i), 3.0, A.is_le, A.mult)
+        s = (4 * x0, 4 * (x0 + n))
+        v("scan", o("uu", *s), o("d0", *s), o("d1", *s), o("uu", 511, 512) if h else 0.0, A.add, A.add)
+    for c in range(8):
+        v("ts", o("bt", 114 * c + 2, 114 * c + 114), o("uu", 7, 896, 8), o("klo", c, c + 1), o("khi", c, c + 1), A.max, A.min)
+    v("scan", o("sc"), o("rsl"), o("bt"), 0.0, A.mult, A.subtract)
+    counts = o("sc", 113, 912, 114)
 
     sent = []
-
-    def token(e, off):
-        pick("xs", 128 * e, 128 * e + 128, "xq", 0, 272, off)
+    for e in order + [me]:
+        for b in range(4):
+            v("ts", blk(o("off2", 8 * e, 8 * e + 8), b), blk(counts, e), 0.125, None, A.mult)
+        last = pick("xs", 128 * e, 128 * e + 128, "xq", 0, 256, o("off2", 8 * e, 8 * e + 8))
         if e != me:
+            after = [last]
             i = place(me, e)
             sent.append(send(e, _cast(o("xl", 128 * i, 128 * i + 128), "u8"), _cast(o("xs", 128 * e, 128 * e + 128), "u8"), "xa%d" % i))
             sent.append(send(e, o("xls", 128 * i, 128 * i + 128), o("xss", 128 * e, 128 * e + 128), "xa%d" % i, o("xs", 128 * e, 128 * e + 128)))
-    for n, e in enumerate(order + [me]):
-        v("tr", o("lt", 160 * e, 160 * e + 160), o("el", 256 * e + 32, 256 * e + 192))
-        if n == 0:
-            after = [wrap("1", 160 * e, 10)]
-            token(e, o("off2a", 0, 8))
-    wrap("", 0, 40)
-    for e in order[1:] + [me]:
-        token(e, o("off2", 10 * e, 10 * e + 8))
 
-    v("set", o("hb", 512, 576), 0.0, extra=after)
-    v("set", o("ut", 8, 512), 0.0, extra=after)
+    for h, n in enumerate((128, 96)):
+        for i in range(3):
+            act(o("sg", 384 * h + i, 384 * h + 3 * n, 3), ps(3 * h + i, n), F.Sign, f(5 + i), -1.0)
+
     for i in range(4):
         v("q", o("wq", 128 * i, 128 * i + 128), o("wqs", 128 * i, 128 * i + 128), o("wt", 512 * i, 512 * i + 512), extra=after)
+    v("set", o("ul"), 0, extra=after)
     v("q", o("uq"), o("uqs"), o("ut"), extra=after)
     pick("ur", 0, 128, "uq", 0, 128, o("ul"))
 
-    def chunk(xc, lo, hlo, hn, hc, hto, banks):
-        for i, b in enumerate(banks):
-            mx(ps(b, 128), o("wq", 128 * i, 128 * i + 128), o("wqs", 128 * i, 128 * i + 128), o(xc, lo, lo + 128), o(xc + "s", lo, lo + 128), True, True)
+    def chunk(xc, lo, hlo, hn, hc, hto, banks, b):
+        for i, k in enumerate(banks):
+            mx(ps(k, 128), o("wq", 128 * i, 128 * i + 128), o("wqs", 128 * i, 128 * i + 128), o(xc, lo, lo + 128), o(xc + "s", lo, lo + 128), True, True)
             out = o("hb", hlo + i, hlo + 512, 4)
             if i % 2 == 0:
-                act(out, ps(b, 128), F.Relu, 0.0, 0.0625)
+                act(out, ps(k, 128), F.Relu, 0.0, 0.0625)
             else:
-                v("ts", out, ps(b, 128), 0.0, 0.0625, A.max, A.mult)
+                v("ts", out, ps(k, 128), 0.0, 0.0625, A.max, A.mult)
         v("q", o(hc, hto, hto + hn), o(hc + "s", hto, hto + hn), o("hb", hlo, hlo + 4 * hn))
+        mx(ps(b, 128), o("ur"), o("urs"), o(hc, hto, hto + 128), o(hc + "s", hto, hto + 128), True, True)
 
-    chunk("xs", 128 * me, 0, 144, "zq", 0, (0, 1, 2, 3))
-    fills = []
-    for t in ("gt", "gtt"):
-        fills.append(act(o(t, 0, 480), o("tokf"), F.Identity, -9e29, 0.0))
-        fills.append(act(o(t, 480, 520), o("tokf", 0, 40), F.Identity, -9e29, 0.0))
-        act(o(t, 520, 528), o("tokf", 0, 8), F.Identity, 9e29, 0.0)
-    mx(ps(0, 128), o("ur"), o("urs"), o("zq", 0, 128), o("zqs", 0, 128), True, True)
-    act(o("gt", 0, 128), ps(0, 128), F.Copy)
-    act(o("gtt", 0, 128), ps(0, 128), F.Copy)
+    chunk("xs", 128 * me, 0, 144, "zq", 0, (6, 7, 0, 1), 2)
+    act(o("gt", 128 * me, 128 * me + 128), ps(2, 128), F.Copy)
+    act(blk(o("qo"), me), blk(ps(2, 128), me), F.Copy)
 
-    rel = [0 if e == me else 128 + 128 * others.index(e) for e in range(4)]
+    v("ts", o("mask"), o("i16"), f(0), None, A.is_equal, extra=after)
+    v("ts", f(12), f(1), 128.0, -1.0, A.mult, A.add, extra=after)
+    for h, n in enumerate((128, 96)):
+        s = (384 * h, 384 * h + 3 * n)
+        v("scan", o("wsc", *s), o("rst3", *s), o("sg", *s), 0.0, A.mult, A.add, extra=after)
+    v("ts", o("nn"), o("wsc", 2, 672, 3), 0.0, None, A.is_gt)
+    v("scan", o("pp"), o("one"), o("nn"), 0.0, A.mult, A.add)
+    for s in ((0, 112), (112, 224)):
+        v("tt", o("zr", *s), o("nn", *s), o("pp", *s), A.mult)
     for e in range(4):
-        act(o("kr", e, 64, 4), o("zero"), F.Identity, float(rel[e] - 1 - 512))
-    v("ts", o("mab", 0, 64), role("cc"), 0.0, None, A.is_equal, extra=after)
-    v("ts", o("mab", 64, 128), role("cc"), 1.0, None, A.is_equal, extra=after)
-    v("ts", o("tk"), role("tp"), 128.5, None, A.is_lt, extra=after)
-    v("tt", o("v2"), role("tp"), o("kr"), A.add, extra=after)
-    v("tt", o("abe", 0, 64), o("mab", 0, 64), o("tk"), A.mult, extra=after)
-    v("tt", o("abe", 64, 128), o("mab", 64, 128), o("tk"), A.mult, extra=after)
-    v("tt", o("pab2", 0, 64), o("abe", 0, 64), o("v2"), A.mult)
-    v("tt", o("pab2", 64, 128), o("abe", 64, 128), o("v2"), A.mult)
-    v("scan", o("t2"), o("rst", 0, 128), o("pab2"), 0.0, A.mult, A.add)
-    v("ts", o("off3"), o("t2", 3, 128, 4), 512.0, None, A.add)
-    v("ts", o("kv2"), o("kv"), f(13), None, A.subtract, extra=after)
-    v("ts", o("kv"), o("kv2"), 0.0, None, A.is_ge, extra=after)
-    v("ts", o("kv3"), o("kv2"), 13.5, None, A.is_lt, extra=after)
-    v("tt", o("kv2"), o("kv"), o("kv3"), A.mult)
-    v("tt", o("ae"), o("abe", 0, 64), o("kv2"), A.mult)
-    v("tt", o("be"), o("abe", 64, 128), o("kv2"), A.mult)
-    v("tt", o("de"), o("ae"), o("be"), A.subtract)
-    v("set", o("wa", 240, 256), 0.0, extra=after)
+        v("tt", o("gz", 128 * e, 128 * e + 128), _ind(o("zr"), o("off2", 8 * e, 8 * e + 8)), o("mask", 0, 128), A.mult)
+    for s in ((0, 256), (256, 512)):
+        v("scan", o("gs", *s), o("rst16"), o("gz", *s), 0.0, A.mult, A.add)
+    gw = o("gs", 15, 512, 16)
+    v("ts", o("ga"), gw, 128.5, 1024.0, A.is_gt, A.mult)
+    v("ts", o("gd"), gw, 0.5, None, A.is_gt)
+    v("tt", o("gb"), gw, o("ga"), A.add)
+    v("ts", o("gc"), o("gb"), f(12), 512.0, A.add, A.min)
+    v("tt", o("gx"), o("gc"), o("gd"), A.mult)
+    for e in range(4):
+        for k, b in enumerate([r for r in range(4) if r != e]):
+            move(3 * e + k, blk(o("gy", 8 * k, 8 * k + 8), e), blk(o("gx", 8 * e, 8 * e + 8), b))
+    v("tt", o("gp", 0, 8), o("gy", 0, 8), o("gy", 8, 16), A.add)
+    v("tt", o("gp", 8, 16), o("gp", 0, 8), o("gy", 16, 24), A.add)
+    v("ts", o("ol3"), counts, 0.375, 2.0, A.mult, A.add, extra=after)
+    v("tt", o("wg"), _ind(o("wsc"), o("ol3")), o("mask", 0, 128), A.mult)
+    v("scan", o("ws"), o("rst16", 0, 128), o("wg"), 0.0, A.mult, A.add)
+    for k in range(2):
+        v("ts", o("gm", 8 * k, 8 * k + 8), o("ws", 15, 128, 16), 3.0 - 2 * k, 520.0, A.not_equal, A.mult)
+        v("tt", o("gl", 8 * k, 8 * k + 8), o("gm", 8 * k, 8 * k + 8), o("gp", 8, 16), A.max)
+    v("copy", o("offl"), o("gl"))
     for k in range(3):
-        v("ts", f(25 + k), f(0), float(16 * k), 2.0, A.add, A.mult, extra=after)
-        v("ts", f(28 + k), f(25 + k), 2.0, None, A.add, extra=after)
-        v("ts", o("bt", 65 * k, 588, 196), o("zero", 0, 3), f(28 + k), -64.0, A.add, A.mult, extra=after)
-    v("set", o("rsl"), 1.0, extra=after)
-    v("set", o("rsl", 0, 196, 65), 0.0, extra=after)
+        v("ts", f(9 + k), f(0), float(16 * k), None, A.add, extra=after)
+    v("set", o("rs2", 0, 384, 128), 0.0, extra=after)
 
     asked = []
-    BANKS = [(4, 5, 6, 7), (0, 1, 2, 3), (4, 5, 6, 3)]
+    BANKS = [((3, 4, 5, 6), 7), ((0, 1, 2, 3), 4), ((5, 6, 7, 0), 1)]
     for n, s in enumerate(order):
         i = others.index(s)
         arrive("xa%d" % i, [s], 2, [o("xl", 128 * i, 128 * i + 128), o("xls", 128 * i, 128 * i + 128)], 2.4, sent[2 * n:2 * n + 2])
-        chunk("xl", 128 * i, 576 + 512 * i, 128, "hq", 128 * i, BANKS[n])
-        b = BANKS[n][0 if n else 3]
-        mx(ps(b, 128), o("hq", 128 * i, 128 * i + 128), o("hqs", 128 * i, 128 * i + 128), o("uq"), o("uqs"), True, True)
-        act(o("qs", i, i + 1), ps(b, 1), F.Copy)
-        k, c = place(me, s), T.cores[s]
-        rid, pid, _ = topo.addr(c)
-        total["sent"] += len(topo.engines(core, c))
-        asked.append(add("p", lambda i=i, k=k, c=c, rid=rid, pid=pid: g.remote_dma(T.dg[128 * k:128 * k + 128, :], T.qs[:, i:i + 1], T.sem.qa, T.sem.sent, pid, rid, topo.mask(core, c)),
-                         [], [o("qs", i, i + 1)], 0.25))
+        chunk("xl", 128 * i, 576 + 512 * i, 128, "hq", 128 * i, *BANKS[n])
+        for h in range(2):
+            v("tr", half(o("qs", 64 * i, 64 * i + 64), h), half(ps(BANKS[n][1], 64, 64 * h), h))
+        k = place(me, s)
+        asked.append(send(s, o("ql", 4 * k, 4 * k + 2), o("qs", 64 * i + 31, 64 * i + 33), "qa%d" % k))
 
-    v("set", o("tab", 256, 288), 0.0, extra=after)
-    v("set", o("tab", 544, 576), 0.0, extra=after)
-    for e in range(4):
-        v("set", _part(f(24), 32 * e), float(rel[e] - 520), extra=after)
-        v("copy", _part(o("offl", 16, 24), 32 * e), _part(o("off2", 10 * e, 10 * e + 8), 32 * e))
-    act(o("own"), o("tokf", 0, 128), F.Identity, f(24))
-    for k in range(2):
-        v("ts", o("tabw", 256 * k, 256 * k + 256, 16), o("t2", 64 * k + 3, 64 * k + 64, 4), 256.0, None, A.add)
-        v("tr", o("tab", 288 * k, 288 * k + 256), o("tabw", 256 * k, 256 * k + 256))
-        act(o("gab2", 128 * k, 128 * k + 128), _ind(o("tab", 288 * k, 288 * k + 272), o("offl", 16, 24)), F.Identity, -264.0)
-    for k, how in enumerate((A.is_equal, A.not_equal)):
-        s = H[k]
-        v("tt", o("isa", *s), o("gab2", 0, 128), o("own"), how, extra=asked)
-        v("tt", o("lab", *s), o("isa", *s), o("gab2", *H[1 - k]), A.mult)
-        act(o("lab2", 160 * k + 16, 160 * k + 144), o("lab", *s), F.Copy)
-        v("tr", o("lt1", *s), o("lab", *s))
-        v("tr", o("lt0", *s), o("lab2", 160 * k + 32, 160 * k + 160))
-        v("ts", o("offl", 8 * k, 8 * k + 8, 2), o("lt1", s[0], s[1], 32), 520.0, None, A.add)
-        v("ts", o("offl", 8 * k + 1, 8 * k + 8, 2), o("lt0", s[0], s[1], 32), 520.0, None, A.add)
-
-    arrive("qa", others, 1, [o("dg")], 1.7, asked)
-    late = []
     for n, e in enumerate(order):
-        i, q = others.index(e), "ys"
-        late.append(dma(q[n % 2], "dgt", lambda e=e: T.gt[32 * e:32 * e + 1, 128:512], lambda: T.dg[:, :], [_part(o("gt", 128, 512), 32 * e)], [o("dg")]))
-        late.append(dma(q[1 - n % 2], "dgt", lambda e=e: T.qo[32 * e:32 * e + 1, :], lambda i=i: T.dg[128 * i:128 * i + 128, :],
-                        [_part(o("qo"), 32 * e)], [o("dg")]))
-    for k in range(8):
-        dma("ys"[k % 2], "dgo", lambda k=k: T.gtt[16 * k:16 * k + 1, 128:512], lambda: T.dg[:, :],
-            [o("gtt", 128 + 48 * k, 176 + 48 * k)], [o("dg")], fills)
+        i = others.index(e)
+        arrive("qa%d" % i, [e], 1, [o("ql", 4 * i, 4 * i + 2)], 1.7, asked[n:n + 1])
+        v("ts", o("rep", 64 * i, 64 * i + 32), o("zero"), o("ql", 4 * i, 4 * i + 1), None, A.add)
+        act(o("rep", 64 * i + 32, 64 * i + 64), o("zero"), F.Identity, o("ql", 4 * i + 1, 4 * i + 2))
+        for h in range(2):
+            for to in range(2):
+                v("tr", half(o("gt", 128 * e + 64 * h, 128 * e + 64 * h + 64), to), half(o("rep", 64 * i, 64 * i + 64), h))
+            v("tr", blk(o("qo", 64 * h, 64 * h + 64), e), blk(o("rep", 64 * i, 64 * i + 64), 2 * h))
     v("tt", o("a1", 0, 128), _ind(o("gt"), o("offl", 0, 8)), o("qo"), A.is_le)
     v("tt", o("a1", 128, 256), _ind(o("gt"), o("offl", 8, 16)), o("qo"), A.is_lt)
-    counted = v("scan", o("a2", 0, 128), o("a1", 0, 128), o("a1", 128, 256), 0.0, A.add, A.add)
-    told = []
-    v("tt", o("vp"), o("a2", 0, 128, 2), o("a2", 1, 128, 2), A.add)
+    v("scan", o("a2"), o("a1", 0, 128), o("a1", 128, 256), 0.0, A.add, A.add)
+    for k in range(3):
+        v("ts", o("bt2", 128 * k, 128 * k + 128), o("a2"), f(9 + k), None, A.is_le)
+    v("scan", o("sc2"), o("rs2"), o("bt2"), 0.0, A.mult, A.add)
+    told, made = [], []
     for n, e in enumerate(order):
-        s, t = (64 * n, 64 * n + 64), 196 * n
-        do("p", "pb", (o("cb", *s), _part(o("vp"), 32 * e, 1), 128))
-        for k in range(3):
-            v("ts", o("bt", t + 65 * k + 1, t + 65 * k + 65), o("cb", *s), f(25 + k), f(28 + k), A.max, A.min)
-        v("scan", o("sc", t, t + 195), o("rsl", 0, 195), o("bt", t, t + 195), 0.0, A.mult, A.subtract)
-        v("ts", o("ls", 4 * e, 4 * e + 3), o("sc", t + 64, t + 195, 65), 127.0, None, A.min)
+        for b in range(4):
+            made.append(v("ts", blk(o("ls", 4 * e, 4 * e + 3), b), blk(o("sc2", 127, 384, 128), e), 127.0, None, A.min))
         i = place(me, e)
         told.append(send(e, o("la", 4 * i, 4 * i + 3), o("ls", 4 * e, 4 * e + 3), "ar%d" % i))
 
-    act(o("gab", 0, 128), _ind(o("gtt"), o("off3", 16, 24)), F.Copy)
-    v("copy", o("gab", 128, 240), _ind(o("gtt"), o("off3", 24, 31)), extra=(counted,))
-    v("tt", o("wa", 0, 128), _ind(o("gtt"), o("off3", 0, 8)), o("gab", 0, 128), A.is_ge, extra=(counted,))
-    v("tt", o("wa", 128, 240), _ind(o("gtt"), o("off3", 8, 15)), o("gab", 128, 240), A.is_ge)
-    quarter = lambda t, h: o(t, 3 + 128 * h, 128 + 128 * h, 4)
-    for s in H:
-        v("tr", o("wat", *s), o("wa", *s))
+    v("tt", o("zm"), o("zr", 0, 224), o("mask", 0, 224), A.mult, extra=asked)
+    v("scan", o("zs2"), o("rst16", 0, 224), o("zm"), 0.0, A.mult, A.add)
+    v("copy", o("offp"), o("zs2", 15, 224, 16))
     for e in range(4):
-        v("tt", o("x4", e, 64, 4), o("wat", 0, 256, 16), o("de", e, 64, 4), A.mult)
-    for h, s in enumerate(H):
-        v("tt", quarter("m2", h), o("x4", 32 * h, 32 * h + 32), o("be", 32 * h, 32 * h + 32), A.add)
-        v("tr", o("n2", *s), o("m2", *s))
-        v("scan", o("rc", *s), ones(*s), o("n2", *s), o("rc", 127, 128) if h else 0.0, A.mult, A.add)
-        v("tr", o("rtr", *s), o("rc", *s))
-
-    for e in range(4):
-        act(o("kz", e, 64, 4), o("zero"), F.Identity, float(-1 - 128 if e == me else 144 + 48 * others.index(e) - 1 - 128))
-    v("q", o("vq"), o("vqs"), o("vt"))
-    v("ts", o("h1"), role("rtr"), 48.5, None, A.is_lt)
-    v("copy", o("xz"), role("rtr"))
-    v("copy", o("xz", me, 64, 4), o("tp", 4 * me + 3, 256, 16))
-    v("tt", o("hm"), role("m2"), o("h1"), A.mult)
-    v("tt", o("z1"), o("xz"), o("kz"), A.add)
-    v("tt", o("z2"), o("z1"), o("hm"), A.mult)
-    v("scan", o("z3"), o("rst", 0, 64), o("z2"), 0.0, A.mult, A.add)
-    v("ts", o("zn"), o("z3", 3, 64, 4), f(13), None, A.mult)
-    v("ts", o("zp"), o("z3", 3, 64, 4), f(3), None, A.mult)
-    v("tt", o("zl"), o("zn", 1, 15), o("zp", 0, 14), A.add)
-    v("ts", o("off5"), o("zl"), 128.0, None, A.add)
-    v("tt", o("w1"), role("m2"), o("ka"), A.mult)
-    v("tt", o("w2"), o("hm"), o("kb"), A.mult)
-    v("tt", o("w3"), o("w2"), o("w1"), A.add)
-    v("scan", o("w4"), o("rst", 0, 64), o("w3"), 0.0, A.mult, A.add)
-    v("ts", o("wnw", 0, 256, 16), o("w4", 3, 64, 4), -100.0, None, A.add)
-    v("tr", o("wnf"), o("wnw"))
-    dma("y", "out", lambda: T.wn[:, :], lambda: T.wnf[16:17, 0:224], [], [o("wnf")])
+        v("set", blk(f(13), e), float(-1 - 128 if e == me else 144 + 48 * others.index(e) - 1 - 128), extra=asked)
+    v("ts", f(14), f(1), -1.0, 99.0, A.mult, A.add, extra=asked)
+    v("ts", f(15), f(1), 2.0, 1.0, A.mult, A.add, extra=asked)
+    v("q", o("vq"), o("vqs"), o("vt"), extra=asked)
+    v("tt", o("a3"), o("a1", 0, 128), o("a1", 128, 256), A.add, extra=made)
+    v("tt", o("cn", 1, 129), o("a3"), o("a2"), A.mult)
+    v("tt", o("g2"), _ind(o("cn"), o("offp")), o("mask", 0, 224), A.mult)
+    v("scan", o("g3"), o("rst16", 0, 224), o("g2"), 0.0, A.mult, A.add)
+    rk = o("g3", 15, 224, 16)
+    v("ts", o("won"), rk, 0.5, None, A.is_gt)
+    v("ts", o("h1"), rk, 48.5, None, A.is_lt)
+    v("ts", o("xz"), rk, f(13), None, A.add)
+    v("ts", blk(o("xz"), me), blk(o("zs2", 15, 224, 16), me), blk(f(13), me), None, A.add)
+    v("tt", o("hm"), o("won"), o("h1"), A.mult)
+    v("ts", o("w1"), o("won"), f(14), None, A.mult)
+    v("tt", o("zw", 0, 14), o("hm"), o("xz"), A.mult)
+    v("ts", o("w2"), o("hm"), f(15), None, A.mult)
+    v("tt", o("zw", 14, 28), o("w1"), o("w2"), A.add)
+    for h in range(2):
+        move(h, half(o("t1"), h), half(o("zw"), 1 - h))
+    v("tt", o("s1"), o("zw"), o("t1"), A.add)
+    for b in range(4):
+        move(b, blk(o("t2"), b), blk(o("s1"), b ^ 1))
+    v("tt", o("s2"), o("s1"), o("t2"), A.add)
+    v("ts", o("off5"), o("s2", 0, 14), 128.0, None, A.add)
+    v("ts", blk(o("wnw", 0, 14), 0), blk(o("s2", 14, 28), 0), -100.0, None, A.add)
+    v("tr", blk(o("wnf"), 0), blk(o("wnw"), 0))
+    dma("y", "out", lambda: T.wn[:, :], lambda: T.wnf[0:14, 0:16], [], [blk(o("wnf"), 0)])
 
     came = []
     for n, s in enumerate(order):

@@ -1,3 +1,4 @@
+import numpy as np
 from concourse.mybir import dt, AluOpType as A, ActivationFunctionType as F
 
 
@@ -5,11 +6,11 @@ def _buffers():
     d = {"ps": ("psum", [128, 4096], "float32")}
     kinds = {
         "bfloat16": "xt 1024 rtt 512 wt 2048 ut 512 vt 512 hb 2112 d0 896 d1 896 uu 896 bt 912 sc 912 rsl 912 "
-                    "i3 672 i16 256 rst3 672 rst16 256 mask 256 one 224 sg 672 wsc 688 nn 224 pp 224 zr 240 gz 512 gs 512 "
+                    "i3 672 i16 256 rst3 672 rst16 256 mask 256 mk0 256 one 224 sg 672 wsc 688 nn 224 pp 224 zr 240 gz 512 gs 512 "
                     "wg 128 ws 128 a1 256 a2 128 a3 128 bt2 384 sc2 384 rs2 384 cn 240 zm 224 zs2 224 g2 224 g3 224",
-        "float32": "ysb 224 sf 32 zero 32 kl0 8 klo 8 khi 8 ga 32 gb 32 gc 32 gd 32 gx 32 gy 24 gp 16 gm 16 gl 16 "
+        "float32": "ysb 224 sf 32 zero 32 kl0 8 klo 8 khi 8 ea 48 ga 32 gb 32 gc 32 gd 32 gx 32 gy 24 gp 16 gm 16 gl 16 "
                    "qs 192 ql 12 rep 192 gt 528 qo 128 won 14 h1 14 hm 14 xz 14 w1 14 w2 14 zw 28 t1 28 s1 28 t2 28 s2 28 wnw 32 wnf 32",
-        "uint16": "sl 20 ul 8 off2 32 ol3 8 offl 16 offp 14 off5 14 ls 16 la 12",
+        "uint16": "sl 20 ul 8 off2 32 offe 32 ol3 8 offl 16 offp 14 off5 14 ls 16 la 12",
         "int32": "si 4 sj 32",
     }
     for t, text in kinds.items():
@@ -27,7 +28,13 @@ SCRATCH = _buffers()
 SEMAPHORES = ["v", "s", "t", "p", "dx", "dx2", "dr", "dw", "du", "dv", "out", "sent", "ha"] \
     + ["xa%d" % i for i in range(3)] + ["qa%d" % i for i in range(3)] + ["ar%d" % i for i in range(3)]
 BIG = 2.0 ** 27
-WAKE, CYC = 0.12, 0.00083
+WAKE, CYC = 0.14, 0.00083
+BYTES = {"float8_e4m3fn_x4": 4, "uint8": 1, "float32": 4, "uint16": 2}
+GUESS = [(.05, .03, 1.0, .1, 1.2, .015, 1 / 30e3, .9, -.3, 0.0), (.1, .015, 1.0, .3, 1.7, .005, 1 / 30e3, .9, 0.0, -.8),
+         (.15, .0, 1.0, .3, 1.4, .015, 1 / 30e3, .9, -.3, 0.0), (.2, .0, 1.0, .1, .8, .005, 1 / 12e3, 1.9, 0.0, .8),
+         (.15, .015, 1.25, .3, 1.8, .02, 1 / 15e3, 1.9, 0.0, .4)]
+ROUNDS, HEAT = 16000, 0.1
+FOUND = {}
 
 
 def _o(name, a=0, z=None, step=1):
@@ -78,38 +85,35 @@ def _cost(name, args):
     return max(64, n * (2 if name == "tt" else .5 if two else 1)) * CYC
 
 
-def _order(ops):
+def _first(ops):
     n = len(ops)
+    deps = [o["deps"] | o["soft"] for o in ops]
     prio = [0.0] * n
     for i in range(n - 1, -1, -1):
         prio[i] += ops[i]["cost"] + ops[i]["lat"]
-        for d in ops[i]["deps"]:
+        for d in deps[i]:
             prio[d] = max(prio[d], prio[i] + WAKE)
-    need = [len(o["deps"]) for o in ops]
+    need = [len(d) for d in deps]
     succ = [[] for o in ops]
-    for i, o in enumerate(ops):
-        for d in o["deps"]:
+    for i in range(n):
+        for d in deps[i]:
             succ[d].append(i)
-    ready, fin, free = [0.0] * n, [0.0] * n, {}
-    can, lists = {}, {}
-
-    def release(i):
-        q = ops[i]["q"]
-        if q is None:
-            finish(i, ready[i])
-        else:
-            can.setdefault(q, []).append(i)
+    ready, free, can, seq = [0.0] * n, {}, {}, []
 
     def finish(i, start):
-        fin[i] = start + ops[i]["cost"] + ops[i]["lat"]
+        seq.append(i)
+        end = start + ops[i]["cost"] + ops[i]["lat"]
         for j in succ[i]:
-            ready[j] = max(ready[j], fin[i] + (WAKE if ops[j]["q"] else 0))
+            ready[j] = max(ready[j], end + (WAKE if ops[j]["q"] else 0))
             need[j] -= 1
             if need[j] == 0:
-                release(j)
+                if ops[j]["q"] is None:
+                    finish(j, ready[j])
+                else:
+                    can.setdefault(ops[j]["q"], []).append(j)
     for i in range(n):
-        if not ops[i]["deps"]:
-            release(i)
+        if not deps[i]:
+            can.setdefault(ops[i]["q"], []).append(i)
     while True:
         best = None
         for q, c in can.items():
@@ -126,12 +130,111 @@ def _order(ops):
             if best is None or m < best[0]:
                 best = (m, q, pick)
         if best is None:
-            break
+            return seq
         m, q, i = best
         can[q].remove(i)
-        lists.setdefault(q, []).append(i)
         free[q] = m + ops[i]["cost"]
         finish(i, m)
+
+
+def _time(rows, seq, guess, why=None):
+    wake, more, times, call, way, row, byte, first, slow, late = guess
+    fin, free, busy, last = [0.0] * len(rows), {}, 0.0, {}
+    for i in seq:
+        q, deps, cost, lat, n = rows[i]
+        if q is None:
+            d = max(deps, key=lambda x: fin[x])
+            fin[i] = fin[d] + 0.05
+            if why is not None:
+                why[i] = d
+            continue
+        t, w = free.get(q, 0.0), last.get(q)
+        for d in deps:
+            if fin[d] + wake > t:
+                t, w = fin[d] + wake, d
+        last[q] = i
+        if why is not None:
+            why[i] = w
+        if n:
+            free[q] = t + call
+            busy = max(busy, t + call + first) + 16 * (row + n * byte)
+            fin[i], first = busy + way, 0.0
+        elif lat:
+            free[q] = t + cost
+            fin[i] = t + cost + lat + slow + (late if lat > 3.1 else 0.0)
+        else:
+            fin[i] = free[q] = t + cost * times + more
+    return fin
+
+
+def _order(ops):
+    n = len(ops)
+    rows = [(o["q"], [d for d in o["deps"] if not (o["q"] == "t" and ops[d]["q"] == "t")], o["cost"], o["lat"], o.get("n", 0)) for o in ops]
+    if n not in FOUND:
+        succ = [[] for o in ops]
+        for i, o in enumerate(ops):
+            for d in o["deps"]:
+                succ[d].append(i)
+        seq = _first(ops)
+        value = lambda s: sum(max(_time(rows, s, x)) for x in GUESS)
+        now = value(seq)
+        best, kept, paths = now, seq, None
+        draws = np.random.default_rng(1).random((ROUNDS, 4)).tolist()
+        for r, (a, b, c, u) in enumerate(draws):
+            if paths is None:
+                paths, pos = [], {x: j for j, x in enumerate(seq)}
+                for x in GUESS:
+                    why = {}
+                    fin = _time(rows, seq, x, why)
+                    i = fin.index(max(fin))
+                    while why[i] is not None:
+                        if why[i] not in ops[i]["deps"]:
+                            paths.append((why[i], i))
+                        i = why[i]
+            if u < 0.5 and paths:
+                j, i = paths[int(a * len(paths))]
+                if b < 0.5:
+                    far = min(pos[i] + 1 + int(80 * b * b), n)
+                    go, part = {j}, seq[pos[j]:far]
+                    for x in part:
+                        if ops[x]["deps"] & go:
+                            go.add(x)
+                    if i in go:
+                        continue
+                    new = seq[:pos[j]] + [x for x in part if x not in go] + [x for x in part if x in go] + seq[far:]
+                else:
+                    near = max(pos[j] - int(80 * (b - .5) ** 2), 0)
+                    go, part = {i}, seq[near:pos[i] + 1]
+                    for x in reversed(part):
+                        if x in go:
+                            go |= ops[x]["deps"]
+                    if j in go:
+                        continue
+                    new = seq[:near] + [x for x in part if x in go] + [x for x in part if x not in go] + seq[pos[i] + 1:]
+            else:
+                k = int(a * n)
+                i = seq[k]
+                lo = max([pos[d] for d in ops[i]["deps"]] + [k - 41, -1]) + 1
+                hi = min([pos[d] for d in succ[i]] + [n, k + 41]) - 1
+                new = seq[:k] + seq[k + 1:]
+                new.insert(lo + int(b * (hi - lo + 1)), i)
+            x = value(new)
+            if x <= now + HEAT * c * (1 - r / ROUNDS) ** 2:
+                seq, now, paths = new, x, None
+                if x < best:
+                    best, kept = x, new
+        FOUND[n] = {x: j for j, x in enumerate(kept)}
+    rank, seq, done = FOUND[n], [], set()
+    left = sorted(range(n), key=lambda i: rank[i])
+    while left:
+        i = next(x for x in left if ops[x]["deps"] <= done)
+        left.remove(i)
+        done.add(i)
+        seq.append(i)
+    lists = {}
+    for i in seq:
+        if ops[i]["q"]:
+            lists.setdefault(ops[i]["q"], []).append(i)
     return lists
 
 
@@ -146,6 +249,7 @@ def rank_program(g, core, T, topo):
         a, b = topo.chip(core), topo.chip(T.cores[r])
         return 2 if topo.mates(a, b) else 1 if topo.same_plane(a, b) else 0
     order = sorted(others, key=far)
+    every = order + [me]
 
     ops, wrote, readers = [], {}, {}
     total = {}
@@ -158,25 +262,26 @@ def rank_program(g, core, T, topo):
             x = x.bitcast(kinds[o[5]])
         return x.indirect(mat(o[6])) if o[6] else x
 
-    def add(q, fn, outs, ins, cost, lat=0.0, sem=None, extra=()):
+    def add(q, fn, outs, ins, cost, lat=0.0, sem=None, extra=(), soft=()):
         i, deps = len(ops), set(extra)
         for o in list(ins) + list(outs):
             if o[6]:
                 ins = list(ins) + [o[6]]
         for o in ins:
-            if o[1] != "ps":
-                for k in _keys(o):
-                    if k in wrote:
-                        deps.add(wrote[k])
-                    readers.setdefault(k, []).append(i)
-        for o in list(outs) + [o for o in ins if o[1] == "ps"]:
+            for k in _keys(o):
+                if k in wrote:
+                    deps.add(wrote[k])
+                if o[1] == "ps":
+                    deps.update(j for j in readers.get(k, ()) if ops[j]["q"] != q)
+                readers.setdefault(k, []).append(i)
+        for o in outs:
             for k in _keys(o):
                 if k in wrote:
                     deps.add(wrote[k])
                 deps.update(readers.pop(k, ()))
                 wrote[k] = i
         deps.discard(i)
-        ops.append({"q": q, "fn": fn, "deps": deps, "cost": cost, "lat": lat, "sem": sem})
+        ops.append({"q": q, "fn": fn, "deps": deps, "soft": set(soft), "cost": cost, "lat": lat, "sem": sem})
         return i
 
     V = g.vector
@@ -184,13 +289,13 @@ def rank_program(g, core, T, topo):
              "scan": V.tensor_tensor_scan, "q": V.quantize_mx, "act": g.scalar.activation, "mx": g.tensor.matmul_mx,
              "iota": lambda *a: g.iota(*a, allow_small_or_imprecise_dtypes=True), "iota32": g.iota}
 
-    def do(q, name, args, extra=()):
+    def do(q, name, args, soft=()):
         k = 2 if name == "q" else 1
         fn = lambda: calls[name](*[mat(a) if _isop(a) else a for a in args])
-        return add(q, fn, args[:k], [a for a in args[k:] if _isop(a)], _cost(name.replace("32", ""), args), 0.0, "own", extra)
+        return add(q, fn, args[:k], [a for a in args[k:] if _isop(a)], _cost(name.replace("32", ""), args), 0.0, "own", (), soft)
 
-    v = lambda name, *args, extra=(): do("v", name, args, extra)
-    act = lambda *args, extra=(): do("s", "act", args, extra)
+    v = lambda name, *args, soft=(): do("v", name, args, soft)
+    act = lambda *args, soft=(): do("s", "act", args, soft)
     mx = lambda *args: do("t", "mx", args)
     iota = lambda *args: do("p", "iota", args)
 
@@ -203,7 +308,9 @@ def rank_program(g, core, T, topo):
         c = T.cores[dst]
         rid, pid, _ = topo.addr(c)
         total["sent"] = total.get("sent", 0) + len(topo.engines(core, c))
-        return add("p", lambda: g.remote_dma(mat(out), mat(in_), T.sem[sem], T.sem["sent"], pid, rid, topo.mask(core, c)), [], [in_] + list(more), 0.25)
+        i = add("p", lambda: g.remote_dma(mat(out), mat(in_), T.sem[sem], T.sem["sent"], pid, rid, topo.mask(core, c)), [], [in_] + list(more), 0.25)
+        ops[i]["n"] = _width(in_) * BYTES[SCRATCH[in_[1]][2]]
+        return i
 
     def arrive(sem, src, writes, outs, lat, extra):
         total[sem] = total.get(sem, 0) + writes * sum(len(topo.engines(T.cores[s], core)) for s in src)
@@ -218,16 +325,17 @@ def rank_program(g, core, T, topo):
     ps = lambda b, n, a=0: _o("ps", 512 * b + a, 512 * b + a + n)
     blk = lambda x, e: _part(x, 32 * e)
     half = lambda x, h: _part(x, 64 * h, 64)
+    fill = lambda out, x: act(out, o("i16", 0, _width(out))[:7] + out[7:], F.Identity, x, 0.0)
 
-    def move(n, out, in_, extra=()):
-        return v("copy", out, in_, extra=extra) if n % 2 == 0 else act(out, in_, F.Copy, extra=extra)
+    def move(n, out, in_):
+        return v("copy", out, in_) if n % 2 == 0 else act(out, in_, F.Copy)
 
-    dma("s", "dr", lambda: T.rtt[:, 0:16], lambda: T.rt[:, 0:16], [o("rtt", 0, 16)], [])
+    dr = dma("s", "dr", lambda: T.rtt[:, 0:16], lambda: T.rt[:, 0:16], [o("rtt", 0, 16)], [])
     dma("y", "dx", lambda: T.xt[:, 0:512], lambda: T.x[:, 0:512], [o("xt", 0, 512)], [], (), 2.6)
-    dx = dma("y", "dx2", lambda: T.xt[:, 512:896], lambda: T.x[:, 512:896], [o("xt", 512, 896)], [], (), 3.0)
-    dma("y", "dw", lambda: T.wt[:, :], lambda: T.w[:, :], [o("wt")], [], (dx,), 4.0)
-    dma("y", "du", lambda: T.ut[:, :], lambda: T.u[:, :], [o("ut")], [], (dx,), 4.3)
-    dma("y", "dv", lambda: T.vt[:, :], lambda: T.v[:, :], [o("vt")], [], (dx,), 4.6)
+    dma("y", "dx2", lambda: T.xt[:, 512:896], lambda: T.x[:, 512:896], [o("xt", 512, 896)], [], (), 3.0)
+    dma("y", "dw", lambda: T.wt[:, :], lambda: T.w[:, :], [o("wt")], [], (dr,), 4.0)
+    dma("y", "du", lambda: T.ut[:, :], lambda: T.u[:, :], [o("ut")], [], (dr,), 4.4)
+    dma("y", "dv", lambda: T.vt[:, :], lambda: T.v[:, :], [o("vt")], [], (dr,), 4.8)
 
     do("p", "iota32", (o("si", 0, 1), [[0, 1]], 0, 1))
     do("p", "iota32", (o("sj", 0, 8), [[1, 4], [0, 2]], 124, 0))
@@ -235,17 +343,18 @@ def rank_program(g, core, T, topo):
     iota(o("kl0"), [[256, 8]], 0, 0)
     iota(o("i16"), [[0, 16], [1, 16]], 0, 0)
     iota(o("i3"), [[0, 224], [1, 3]], 0, 0)
-    iota(o("cn"), [[0, 240]], 0, 0)
     v("set", o("rtt", 16, 496), 0.0)
     v("set", o("xt", 896, 1024), 0.0)
+    v("set", o("ul"), 0)
     v("ts", o("sj", 8, 20), o("sj", 20, 32), 3, None, A.bitwise_and)
     v("copy", o("sl"), o("sj", 0, 20))
     v("ts", o("si", 1, 2), o("si", 0, 1), 15, None, A.bitwise_and)
     v("ts", o("si", 2, 3), o("si", 0, 1), 5, None, A.logical_shift_right)
-    v("copy", o("sf", 0, 2), o("si", 1, 3))
+    v("ts", o("si", 3, 4), o("si", 0, 1), 16, 4, A.bitwise_and, A.logical_shift_right)
+    v("copy", o("sf", 0, 3), o("si", 1, 4))
     for i in (1, 2, 3):
-        v("ts", f(1 + i), f(1), 3.5 - i, -1e-30, A.is_gt, A.mult)
-    v("ts", o("sf", 5, 8), o("sf", 2, 5), 2.0, 1e-30, A.mult, A.add)
+        v("ts", f(15 + i), f(1), 3.5 - i, -1e-30, A.is_gt, A.mult)
+    v("ts", o("sf", 19, 22), o("sf", 16, 19), 2.0, 1e-30, A.mult, A.add)
     v("ts", f(8), f(0), 16.0, None, A.mult)
     v("ts", o("klo"), o("kl0"), f(8), None, A.add)
     v("ts", o("khi"), o("kl0"), f(8), 16.0, A.add, A.add)
@@ -259,15 +368,25 @@ def rank_program(g, core, T, topo):
         v("set", o("d1", k, 896, 8), x)
     act(o("rst3"), o("i3"), F.Sign)
     act(o("rst16"), o("i16"), F.Sign)
-    act(o("one"), o("i16", 0, 224), F.Identity, 1.0, 0.0)
-    act(o("rs2"), o("i3", 0, 384), F.Identity, 1.0, 0.0)
-    act(o("zero"), o("i16", 0, 32), F.Identity, 0.0, 0.0)
-    act(o("wnw"), o("i16", 0, 32), F.Identity, 0.0, 0.0)
-    act(o("zr", 224, 240), o("i16", 0, 16), F.Identity, 0.0, 0.0)
-    act(o("wsc", 672, 688), o("i16", 0, 16), F.Identity, 0.0, 0.0)
-    act(o("hb", 512, 576), o("i16", 0, 64), F.Identity, 0.0, 0.0)
-    act(o("gt", 512, 520), o("i16", 0, 8), F.Identity, -9e29, 0.0)
-    act(o("gt", 520, 528), o("i16", 0, 8), F.Identity, 9e29, 0.0)
+    act(f(4), f(0), F.Identity, 0.0, -1.0)
+    act(o("mk0"), o("i16"), F.Abs, f(4))
+    act(o("mask"), o("mk0"), F.Relu, 1.0, -1.0)
+    act(f(3), f(2), F.Identity, 1.0, -1.0)
+    for k in range(3):
+        act(f(9 + k), f(0), F.Identity, float(16 * k))
+    act(f(12), f(1), F.Identity, -1.0, 128.0)
+    for e in every:
+        fill(blk(f(13), e), float(-1 - 128 if e == me else 144 + 48 * others.index(e) - 1 - 128))
+    act(f(14), f(1), F.Identity, 99.0, -1.0)
+    act(f(15), f(1), F.Identity, 1.0, 2.0)
+    fill(o("one"), 1.0)
+    fill(o("rs2", 0, 192), 1.0)
+    fill(o("rs2", 192, 384), 1.0)
+    fill(o("rs2", 0, 384, 128), 0.0)
+    for x in (o("zero"), o("wnw"), o("zr", 224, 240), o("wsc", 672, 688), o("hb", 512, 576), o("cn")):
+        fill(x, 0.0)
+    fill(o("gt", 512, 520), -9e29)
+    fill(o("gt", 520, 528), 9e29)
 
     v("ts", o("rtt", 496, 512), o("rtt", 0, 16), -1.0, None, A.mult)
     v("q", o("rq"), o("rqs"), o("rtt", 0, 512))
@@ -283,7 +402,7 @@ def rank_program(g, core, T, topo):
                 lo = 0 if first else 128 + 32 * i
                 mx(ps(3 * h + i, 128), o("rr", lo, lo + 128), o("rrs", lo, lo + 128), o("xq", x0, x0 + 128), o("xqs", x0, x0 + 128), first, not first)
         for i, (name, k) in enumerate(spot):
-            v("ts", o(name, 4 * x0 + k, 4 * (x0 + n), 4), ps(3 * h + i, n), f(2 + i), 3.0, A.is_le, A.mult)
+            v("ts", o(name, 4 * x0 + k, 4 * (x0 + n), 4), ps(3 * h + i, n), f(16 + i), 3.0, A.is_le, A.mult)
         s = (4 * x0, 4 * (x0 + n))
         v("scan", o("uu", *s), o("d0", *s), o("d1", *s), o("uu", 511, 512) if h else 0.0, A.add, A.add)
     for c in range(8):
@@ -292,7 +411,7 @@ def rank_program(g, core, T, topo):
     counts = o("sc", 113, 912, 114)
 
     sent = []
-    for e in order + [me]:
+    for e in every:
         for b in range(4):
             v("ts", blk(o("off2", 8 * e, 8 * e + 8), b), blk(counts, e), 0.125, None, A.mult)
         last = pick("xs", 128 * e, 128 * e + 128, "xq", 0, 256, o("off2", 8 * e, 8 * e + 8))
@@ -304,84 +423,86 @@ def rank_program(g, core, T, topo):
 
     for h, n in enumerate((128, 96)):
         for i in range(3):
-            act(o("sg", 384 * h + i, 384 * h + 3 * n, 3), ps(3 * h + i, n), F.Sign, f(5 + i), -1.0)
+            act(o("sg", 384 * h + i, 384 * h + 3 * n, 3), ps(3 * h + i, n), F.Sign, f(19 + i), -1.0)
 
     for i in range(4):
-        v("q", o("wq", 128 * i, 128 * i + 128), o("wqs", 128 * i, 128 * i + 128), o("wt", 512 * i, 512 * i + 512), extra=after)
-    v("set", o("ul"), 0, extra=after)
-    v("q", o("uq"), o("uqs"), o("ut"), extra=after)
+        v("q", o("wq", 128 * i, 128 * i + 128), o("wqs", 128 * i, 128 * i + 128), o("wt", 512 * i, 512 * i + 512), soft=after)
+    v("q", o("uq"), o("uqs"), o("ut"), soft=after)
     pick("ur", 0, 128, "uq", 0, 128, o("ul"))
 
     def chunk(xc, lo, hlo, hn, hc, hto, banks, b):
         for i, k in enumerate(banks):
             mx(ps(k, 128), o("wq", 128 * i, 128 * i + 128), o("wqs", 128 * i, 128 * i + 128), o(xc, lo, lo + 128), o(xc + "s", lo, lo + 128), True, True)
             out = o("hb", hlo + i, hlo + 512, 4)
-            if i % 2 == 0:
+            if i % 2 == 0 or hc == "zq":
                 act(out, ps(k, 128), F.Relu, 0.0, 0.0625)
             else:
                 v("ts", out, ps(k, 128), 0.0, 0.0625, A.max, A.mult)
         v("q", o(hc, hto, hto + hn), o(hc + "s", hto, hto + hn), o("hb", hlo, hlo + 4 * hn))
         mx(ps(b, 128), o("ur"), o("urs"), o(hc, hto, hto + 128), o(hc + "s", hto, hto + 128), True, True)
 
-    chunk("xs", 128 * me, 0, 144, "zq", 0, (6, 7, 0, 1), 2)
-    act(o("gt", 128 * me, 128 * me + 128), ps(2, 128), F.Copy)
-    act(blk(o("qo"), me), blk(ps(2, 128), me), F.Copy)
-
-    v("ts", o("mask"), o("i16"), f(0), None, A.is_equal, extra=after)
-    v("ts", f(12), f(1), 128.0, -1.0, A.mult, A.add, extra=after)
-    for h, n in enumerate((128, 96)):
-        s = (384 * h, 384 * h + 3 * n)
-        v("scan", o("wsc", *s), o("rst3", *s), o("sg", *s), 0.0, A.mult, A.add, extra=after)
-    v("ts", o("nn"), o("wsc", 2, 672, 3), 0.0, None, A.is_gt)
-    v("scan", o("pp"), o("one"), o("nn"), 0.0, A.mult, A.add)
-    for s in ((0, 112), (112, 224)):
-        v("tt", o("zr", *s), o("nn", *s), o("pp", *s), A.mult)
-    for e in range(4):
-        v("tt", o("gz", 128 * e, 128 * e + 128), _ind(o("zr"), o("off2", 8 * e, 8 * e + 8)), o("mask", 0, 128), A.mult)
-    for s in ((0, 256), (256, 512)):
-        v("scan", o("gs", *s), o("rst16"), o("gz", *s), 0.0, A.mult, A.add)
-    gw = o("gs", 15, 512, 16)
-    v("ts", o("ga"), gw, 128.5, 1024.0, A.is_gt, A.mult)
-    v("ts", o("gd"), gw, 0.5, None, A.is_gt)
-    v("tt", o("gb"), gw, o("ga"), A.add)
-    v("ts", o("gc"), o("gb"), f(12), 512.0, A.add, A.min)
-    v("tt", o("gx"), o("gc"), o("gd"), A.mult)
-    for e in range(4):
-        for k, b in enumerate([r for r in range(4) if r != e]):
-            move(3 * e + k, blk(o("gy", 8 * k, 8 * k + 8), e), blk(o("gx", 8 * e, 8 * e + 8), b))
-    v("tt", o("gp", 0, 8), o("gy", 0, 8), o("gy", 8, 16), A.add)
-    v("tt", o("gp", 8, 16), o("gp", 0, 8), o("gy", 16, 24), A.add)
-    v("ts", o("ol3"), counts, 0.375, 2.0, A.mult, A.add, extra=after)
-    v("tt", o("wg"), _ind(o("wsc"), o("ol3")), o("mask", 0, 128), A.mult)
-    v("scan", o("ws"), o("rst16", 0, 128), o("wg"), 0.0, A.mult, A.add)
-    for k in range(2):
-        v("ts", o("gm", 8 * k, 8 * k + 8), o("ws", 15, 128, 16), 3.0 - 2 * k, 520.0, A.not_equal, A.mult)
-        v("tt", o("gl", 8 * k, 8 * k + 8), o("gm", 8 * k, 8 * k + 8), o("gp", 8, 16), A.max)
-    v("copy", o("offl"), o("gl"))
-    for k in range(3):
-        v("ts", f(9 + k), f(0), float(16 * k), None, A.add, extra=after)
-    v("set", o("rs2", 0, 384, 128), 0.0, extra=after)
-
     asked = []
-    BANKS = [((3, 4, 5, 6), 7), ((0, 1, 2, 3), 4), ((5, 6, 7, 0), 1)]
+    BANKS = [((6, 7, 0, 1), 2), ((3, 4, 5, 6), 7), ((0, 1, 2, 3), 4)]
     for n, s in enumerate(order):
         i = others.index(s)
-        arrive("xa%d" % i, [s], 2, [o("xl", 128 * i, 128 * i + 128), o("xls", 128 * i, 128 * i + 128)], 2.4, sent[2 * n:2 * n + 2])
+        arrive("xa%d" % i, [s], 2, [o("xl", 128 * i, 128 * i + 128), o("xls", 128 * i, 128 * i + 128)], 2.3, sent[2 * n:2 * n + 2])
         chunk("xl", 128 * i, 576 + 512 * i, 128, "hq", 128 * i, *BANKS[n])
         for h in range(2):
             v("tr", half(o("qs", 64 * i, 64 * i + 64), h), half(ps(BANKS[n][1], 64, 64 * h), h))
         k = place(me, s)
         asked.append(send(s, o("ql", 4 * k, 4 * k + 2), o("qs", 64 * i + 31, 64 * i + 33), "qa%d" % k))
 
+    chunk("xs", 128 * me, 0, 144, "zq", 0, (5, 6, 7, 0), 1)
+    act(o("gt", 128 * me, 128 * me + 128), ps(1, 128), F.Copy)
+    act(blk(o("qo"), me), blk(ps(1, 128), me), F.Copy)
+
+    for h, n in enumerate((128, 96)):
+        s = (384 * h, 384 * h + 3 * n)
+        v("scan", o("wsc", *s), o("rst3", *s), o("sg", *s), 0.0, A.mult, A.add, soft=after)
+    v("ts", o("nn"), o("wsc", 2, 672, 3), 0.0, None, A.is_gt)
+    v("scan", o("pp"), o("one"), o("nn"), 0.0, A.mult, A.add)
+    for s in ((0, 112), (112, 224)):
+        v("tt", o("zr", *s), o("nn", *s), o("pp", *s), A.mult)
+    v("ts", o("ea", 0, 16), o("off2", 0, 32, 2), f(3), None, A.mult, soft=after)
+    v("ts", o("ea", 16, 32), o("off2", 1, 32, 2), f(2), None, A.mult, soft=after)
+    v("tt", o("ea", 32, 48), o("ea", 0, 16), o("ea", 16, 32), A.add)
+    for k in range(2):
+        v("copy", o("offe", k, 32, 2), o("ea", 32, 48))
+    for e in range(4):
+        act(o("gz", 128 * e, 128 * e + 128), _ind(o("zr"), o("offe", 8 * e, 8 * e + 8)), F.Copy)
+    for s in ((0, 256), (256, 512)):
+        v("tr", o("gs", *s), o("gz", *s))
+    gw = o("gs", 0, 512, 16)
+    v("ts", o("ga"), gw, 128.5, 1024.0, A.is_gt, A.mult)
+    v("ts", o("gd"), gw, 0.5, None, A.is_gt)
+    v("tt", o("gb"), gw, o("ga"), A.add)
+    v("ts", o("gc"), o("gb"), f(12), 512.0, A.add, A.min)
+    v("tt", o("gx"), o("gc"), o("gd"), A.mult)
+    for e in every:
+        for k, b in enumerate([r for r in every if r != e]):
+            move(1 if k else 0, blk(o("gy", 8 * k, 8 * k + 8), e), blk(o("gx", 8 * e, 8 * e + 8), b))
+    v("tt", o("gp", 0, 8), o("gy", 0, 8), o("gy", 8, 16), A.add)
+    v("tt", o("gp", 8, 16), o("gp", 0, 8), o("gy", 16, 24), A.add)
+    v("ts", o("ol3"), counts, 0.375, 2.0, A.mult, A.add, soft=after)
+    v("tt", o("wg"), _ind(o("wsc"), o("ol3")), o("mask", 0, 128), A.mult)
+    v("scan", o("ws"), o("rst16", 0, 128), o("wg"), 0.0, A.mult, A.add)
+    for k in range(2):
+        v("ts", o("gm", 8 * k, 8 * k + 8), o("ws", 15, 128, 16), 3.0 - 2 * k, 520.0, A.not_equal, A.mult)
+        v("tt", o("gl", 8 * k, 8 * k + 8), o("gm", 8 * k, 8 * k + 8), o("gp", 8, 16), A.max)
+    v("copy", o("offl"), o("gl"))
+
     for n, e in enumerate(order):
         i = others.index(e)
-        arrive("qa%d" % i, [e], 1, [o("ql", 4 * i, 4 * i + 2)], 1.7, asked[n:n + 1])
+        arrive("qa%d" % i, [e], 1, [o("ql", 4 * i, 4 * i + 2)], 1.6, asked[n:n + 1])
         v("ts", o("rep", 64 * i, 64 * i + 32), o("zero"), o("ql", 4 * i, 4 * i + 1), None, A.add)
         act(o("rep", 64 * i + 32, 64 * i + 64), o("zero"), F.Identity, o("ql", 4 * i + 1, 4 * i + 2))
         for h in range(2):
             for to in range(2):
                 v("tr", half(o("gt", 128 * e + 64 * h, 128 * e + 64 * h + 64), to), half(o("rep", 64 * i, 64 * i + 64), h))
-            v("tr", blk(o("qo", 64 * h, 64 * h + 64), e), blk(o("rep", 64 * i, 64 * i + 64), 2 * h))
+            if n == 2:
+                v("tr", blk(o("qo", 64 * h, 64 * h + 64), e), blk(o("rep", 64 * i, 64 * i + 64), 2 * h))
+        if n < 2:
+            act(blk(o("qo"), e), blk(o("gt", 128 * e, 128 * e + 128), e), F.Copy)
     v("tt", o("a1", 0, 128), _ind(o("gt"), o("offl", 0, 8)), o("qo"), A.is_le)
     v("tt", o("a1", 128, 256), _ind(o("gt"), o("offl", 8, 16)), o("qo"), A.is_lt)
     v("scan", o("a2"), o("a1", 0, 128), o("a1", 128, 256), 0.0, A.add, A.add)
@@ -395,15 +516,11 @@ def rank_program(g, core, T, topo):
         i = place(me, e)
         told.append(send(e, o("la", 4 * i, 4 * i + 3), o("ls", 4 * e, 4 * e + 3), "ar%d" % i))
 
-    v("tt", o("zm"), o("zr", 0, 224), o("mask", 0, 224), A.mult, extra=asked)
+    v("tt", o("zm"), o("zr", 0, 224), o("mask", 0, 224), A.mult, soft=made)
     v("scan", o("zs2"), o("rst16", 0, 224), o("zm"), 0.0, A.mult, A.add)
     v("copy", o("offp"), o("zs2", 15, 224, 16))
-    for e in range(4):
-        v("set", blk(f(13), e), float(-1 - 128 if e == me else 144 + 48 * others.index(e) - 1 - 128), extra=asked)
-    v("ts", f(14), f(1), -1.0, 99.0, A.mult, A.add, extra=asked)
-    v("ts", f(15), f(1), 2.0, 1.0, A.mult, A.add, extra=asked)
-    v("q", o("vq"), o("vqs"), o("vt"), extra=asked)
-    v("tt", o("a3"), o("a1", 0, 128), o("a1", 128, 256), A.add, extra=made)
+    v("q", o("vq"), o("vqs"), o("vt"), soft=made)
+    v("tt", o("a3"), o("a1", 0, 128), o("a1", 128, 256), A.add, soft=made)
     v("tt", o("cn", 1, 129), o("a3"), o("a2"), A.mult)
     v("tt", o("g2"), _ind(o("cn"), o("offp")), o("mask", 0, 224), A.mult)
     v("scan", o("g3"), o("rst16", 0, 224), o("g2"), 0.0, A.mult, A.add)
@@ -431,13 +548,13 @@ def rank_program(g, core, T, topo):
     came = []
     for n, s in enumerate(order):
         i = others.index(s)
-        arrive("ar%d" % i, [s], 1, [o("la", 4 * i, 4 * i + 3)], 1.7, told[n:n + 1])
+        arrive("ar%d" % i, [s], 1, [o("la", 4 * i, 4 * i + 3)], 1.6, told[n:n + 1])
         pick("hs", 48 * i, 48 * i + 48, "hq", 128 * i, 128 * i + 128, o("la", 4 * i, 4 * i + 3))
         k = 144 + 48 * place(me, s)
         came.append(send(s, _cast(o("zq", k, k + 48), "u8"), _cast(o("hs", 48 * i, 48 * i + 48), "u8"), "ha"))
         came.append(send(s, o("zqs", k, k + 48), o("hss", 48 * i, 48 * i + 48), "ha", o("hs", 48 * i, 48 * i + 48)))
 
-    arrive("ha", others, 2, [o("zq", 144, 288), o("zqs", 144, 288)], 2.0, came)
+    arrive("ha", others, 2, [o("zq", 144, 288), o("zqs", 144, 288)], 1.8, came)
     pick("z", 0, 128, "zq", 0, 288, o("off5", 0, 8))
     pick("z", 128, 224, "zq", 0, 288, o("off5", 8, 14))
     mx(ps(0, 128), o("vq"), o("vqs"), o("z", 0, 128), o("zs", 0, 128), True, True)
@@ -448,7 +565,7 @@ def rank_program(g, core, T, topo):
     for k in range(4):
         dma("s" if k % 2 == 0 else "y", "out", lambda k=k: T.osc[4 * k:4 * k + 4, :], lambda k=k: T.zs[32 * k:32 * k + 4, :], [], [o("zs")])
     for a, z in ((0, 128), (128, 224)):
-        dma("y", "out", lambda a=a, z=z: T.y[:, a:z], lambda a=a, z=z: T.ysb[:, a:z], [], [o("ysb", a, z)])
+        dma("s" if a else "y", "out", lambda a=a, z=z: T.y[:, a:z], lambda a=a, z=z: T.ysb[:, a:z], [], [o("ysb", a, z)])
 
     queue = {"v": V, "s": g.scalar, "t": g.tensor, "p": g, "y": g.sync}
     lists = _order(ops)

import numpy as np
from concourse.mybir import dt, AluOpType as A, ActivationFunctionType as F


def _buffers():
    d = {"ps": ("psum", [128, 4096], "float32")}
    kinds = {
        "bfloat16": "xt 1024 rtt 512 wt 2048 ut 512 vt 512 hb 2112 d0 896 d1 896 uu 896 bt 912 sc 912 rsl 912 "
                    "i3 672 i16 256 rst3 672 rst16 256 mask 256 mk0 256 one 224 sg 672 wsc 688 nn 224 pp 224 zr 240 gz 512 gs 512 "
                    "wg 128 ws 128 a1 256 a2 128 a3 128 bt2 384 sc2 384 rs2 384 cn 240 zm 224 zs2 224 g2 224 g3 224",
        "float32": "ysb 224 sf 32 zero 32 kl0 8 klo 8 khi 8 ea 48 ga 32 gb 32 gc 32 gd 32 gx 32 gy 24 gp 16 gm 16 gl 16 "
                   "qs 192 ql 12 rep 192 gt 528 qo 128 won 14 h1 14 hm 14 xz 14 w1 14 w2 14 zw 28 t1 28 s1 28 t2 28 s2 28 wnw 32 wnf 32",
        "uint16": "sl 20 ul 8 off2 32 offe 32 ol3 8 offl 16 offp 14 off5 14 ls 16 la 12",
        "int32": "si 4 sj 32",
    }
    for t, text in kinds.items():
        w = text.split()
        for name, n in zip(w[::2], w[1::2]):
            d[name] = ("sbuf", [128, int(n)], t)
    w = "xq 256 rq 128 rr 320 wq 512 uq 128 ur 128 vq 128 xs 512 xl 384 hq 384 hs 144 zq 288 z 224".split()
    for name, n in zip(w[::2], w[1::2]):
        d[name] = ("sbuf", [128, int(n)], "float8_e4m3fn_x4")
        d[name + "s"] = ("sbuf", [128, int(n)], "uint8")
    return d


SCRATCH = _buffers()
SEMAPHORES = ["v", "s", "t", "p", "dx", "dx2", "dr", "dw", "du", "dv", "out", "sent", "ha"] \
    + ["xa%d" % i for i in range(3)] + ["qa%d" % i for i in range(3)] + ["ar%d" % i for i in range(3)]
BIG = 2.0 ** 27
WAKE, CYC = 0.14, 0.00083
BYTES = {"float8_e4m3fn_x4": 4, "uint8": 1, "float32": 4, "uint16": 2}
GUESS = [(.05, .03, 1.0, .1, 1.2, .015, 1 / 30e3, .9, -.3, 0.0), (.1, .015, 1.0, .3, 1.7, .005, 1 / 30e3, .9, 0.0, -.8),
         (.15, .0, 1.0, .3, 1.4, .015, 1 / 30e3, .9, -.3, 0.0), (.2, .0, 1.0, .1, .8, .005, 1 / 12e3, 1.9, 0.0, .8),
         (.15, .015, 1.25, .3, 1.8, .02, 1 / 15e3, 1.9, 0.0, .4)]
ROUNDS, HEAT = 16000, 0.1
FOUND = {}


def _o(name, a=0, z=None, step=1):
    return ("@", name, a, SCRATCH[name][1][1] if z is None else z, step, None, None, None)


def _cast(o, how):
    return o[:5] + (how,) + o[6:]


def _ind(o, off):
    return o[:6] + (off, o[7])


def _part(o, p, n=32):
    return o[:7] + ((p, p + n),)


def _keys(o):
    if o[1] == "ps":
        return [("ps", b) for b in range(o[2] // 512, (o[3] - 1) // 512 + 1)]
    blocks = range(o[7][0] // 32, (o[7][1] - 1) // 32 + 1) if o[7] else range(4)
    return [(o[1], c, b) for c in range(o[2], o[3], o[4]) for b in blocks]


def _isop(x):
    return isinstance(x, tuple) and len(x) == 8 and x[0] == "@"


def _width(o):
    return 16 * (o[6][3] - o[6][2]) if o[6] else len(range(o[2], o[3], o[4]))


def _cost(name, args):
    out, n = args[0], _width(args[0])
    if name == "mx":
        return (n + 16) * CYC
    if name == "q":
        return .012 + .00088 * n
    ops = [a for a in args if _isop(a)]
    if name == "iota":
        return .13 + 2 * n * CYC
    if name == "act":
        return .065 + n * CYC * (1.5 if args[1][6] else 1)
    if any(a[6] for a in ops):
        return .05 + 1.6 * n * CYC
    two = all(SCRATCH[a[1]][2] in ("bfloat16", "uint16") for a in ops if _width(a) > 1)
    return max(64, n * (2 if name == "tt" else .5 if two else 1)) * CYC


def _first(ops):
    n = len(ops)
    deps = [o["deps"] | o["soft"] for o in ops]
    prio = [0.0] * n
    for i in range(n - 1, -1, -1):
        prio[i] += ops[i]["cost"] + ops[i]["lat"]
        for d in deps[i]:
            prio[d] = max(prio[d], prio[i] + WAKE)
    need = [len(d) for d in deps]
    succ = [[] for o in ops]
    for i in range(n):
        for d in deps[i]:
            succ[d].append(i)
    ready, free, can, seq = [0.0] * n, {}, {}, []

    def finish(i, start):
        seq.append(i)
        end = start + ops[i]["cost"] + ops[i]["lat"]
        for j in succ[i]:
            ready[j] = max(ready[j], end + (WAKE if ops[j]["q"] else 0))
            need[j] -= 1
            if need[j] == 0:
                if ops[j]["q"] is None:
                    finish(j, ready[j])
                else:
                    can.setdefault(ops[j]["q"], []).append(j)
    for i in range(n):
        if not deps[i]:
            can.setdefault(ops[i]["q"], []).append(i)
    while True:
        best = None
        for q, c in can.items():
            if not c:
                continue
            t = free.get(q, 0.0)
            m = min(max(t, ready[i]) for i in c)
            pick = max((i for i in c if max(t, ready[i]) <= m + 1e-9), key=lambda i: prio[i])
            for d in sorted(c, key=lambda i: -prio[i]):
                e = max(t, ready[d])
                if prio[d] > prio[pick] and e - m < m + ops[pick]["cost"] - e:
                    pick, m = d, e
                    break
            if best is None or m < best[0]:
                best = (m, q, pick)
        if best is None:
            return seq
        m, q, i = best
        can[q].remove(i)
        free[q] = m + ops[i]["cost"]
        finish(i, m)


def _time(rows, seq, guess, why=None):
    wake, more, times, call, way, row, byte, first, slow, late = guess
    fin, free, busy, last = [0.0] * len(rows), {}, 0.0, {}
    for i in seq:
        q, deps, cost, lat, n = rows[i]
        if q is None:
            d = max(deps, key=lambda x: fin[x])
            fin[i] = fin[d] + 0.05
            if why is not None:
                why[i] = d
            continue
        t, w = free.get(q, 0.0), last.get(q)
        for d in deps:
            if fin[d] + wake > t:
                t, w = fin[d] + wake, d
        last[q] = i
        if why is not None:
            why[i] = w
        if n:
            free[q] = t + call
            busy = max(busy, t + call + first) + 16 * (row + n * byte)
            fin[i], first = busy + way, 0.0
        elif lat:
            free[q] = t + cost
            fin[i] = t + cost + lat + slow + (late if lat > 3.1 else 0.0)
        else:
            fin[i] = free[q] = t + cost * times + more
    return fin


def _order(ops):
    n = len(ops)
    rows = [(o["q"], [d for d in o["deps"] if not (o["q"] == "t" and ops[d]["q"] == "t")], o["cost"], o["lat"], o.get("n", 0)) for o in ops]
    if n not in FOUND:
        succ = [[] for o in ops]
        for i, o in enumerate(ops):
            for d in o["deps"]:
                succ[d].append(i)
        seq = _first(ops)
        value = lambda s: sum(max(_time(rows, s, x)) for x in GUESS)
        now = value(seq)
        best, kept, paths = now, seq, None
        draws = np.random.default_rng(1).random((ROUNDS, 4)).tolist()
        for r, (a, b, c, u) in enumerate(draws):
            if paths is None:
                paths, pos = [], {x: j for j, x in enumerate(seq)}
                for x in GUESS:
                    why = {}
                    fin = _time(rows, seq, x, why)
                    i = fin.index(max(fin))
                    while why[i] is not None:
                        if why[i] not in ops[i]["deps"]:
                            paths.append((why[i], i))
                        i = why[i]
            if u < 0.5 and paths:
                j, i = paths[int(a * len(paths))]
                if b < 0.5:
                    far = min(pos[i] + 1 + int(80 * b * b), n)
                    go, part = {j}, seq[pos[j]:far]
                    for x in part:
                        if ops[x]["deps"] & go:
                            go.add(x)
                    if i in go:
                        continue
                    new = seq[:pos[j]] + [x for x in part if x not in go] + [x for x in part if x in go] + seq[far:]
                else:
                    near = max(pos[j] - int(80 * (b - .5) ** 2), 0)
                    go, part = {i}, seq[near:pos[i] + 1]
                    for x in reversed(part):
                        if x in go:
                            go |= ops[x]["deps"]
                    if j in go:
                        continue
                    new = seq[:near] + [x for x in part if x in go] + [x for x in part if x not in go] + seq[pos[i] + 1:]
            else:
                k = int(a * n)
                i = seq[k]
                lo = max([pos[d] for d in ops[i]["deps"]] + [k - 41, -1]) + 1
                hi = min([pos[d] for d in succ[i]] + [n, k + 41]) - 1
                new = seq[:k] + seq[k + 1:]
                new.insert(lo + int(b * (hi - lo + 1)), i)
            x = value(new)
            if x <= now + HEAT * c * (1 - r / ROUNDS) ** 2:
                seq, now, paths = new, x, None
                if x < best:
                    best, kept = x, new
        FOUND[n] = {x: j for j, x in enumerate(kept)}
    rank, seq, done = FOUND[n], [], set()
    left = sorted(range(n), key=lambda i: rank[i])
    while left:
        i = next(x for x in left if ops[x]["deps"] <= done)
        left.remove(i)
        done.add(i)
        seq.append(i)
    lists = {}
    for i in seq:
        if ops[i]["q"]:
            lists.setdefault(ops[i]["q"], []).append(i)
    return lists


def rank_program(g, core, T, topo):
    me = T.rank_of(core)
    if me is None:
        return
    others = [r for r in range(4) if r != me]
    place = lambda src, dst: [r for r in range(4) if r != dst].index(src)

    def far(r):
        a, b = topo.chip(core), topo.chip(T.cores[r])
        return 2 if topo.mates(a, b) else 1 if topo.same_plane(a, b) else 0
    order = sorted(others, key=far)
    every = order + [me]

    ops, wrote, readers = [], {}, {}
    total = {}
    kinds = {"u8": dt.uint8, "u32": dt.uint32}

    def mat(o):
        p, z = o[7] or (0, SCRATCH[o[1]][1][0])
        x = T[o[1]][p:z, o[2]:o[3]] if o[4] == 1 else T[o[1]][p:z, o[2]:o[3]:o[4]]
        if o[5]:
            x = x.bitcast(kinds[o[5]])
        return x.indirect(mat(o[6])) if o[6] else x

    def add(q, fn, outs, ins, cost, lat=0.0, sem=None, extra=(), soft=()):
        i, deps = len(ops), set(extra)
        for o in list(ins) + list(outs):
            if o[6]:
                ins = list(ins) + [o[6]]
        for o in ins:
            for k in _keys(o):
                if k in wrote:
                    deps.add(wrote[k])
                if o[1] == "ps":
                    deps.update(j for j in readers.get(k, ()) if ops[j]["q"] != q)
                readers.setdefault(k, []).append(i)
        for o in outs:
            for k in _keys(o):
                if k in wrote:
                    deps.add(wrote[k])
                deps.update(readers.pop(k, ()))
                wrote[k] = i
        deps.discard(i)
        ops.append({"q": q, "fn": fn, "deps": deps, "soft": set(soft), "cost": cost, "lat": lat, "sem": sem})
        return i

    V = g.vector
    calls = {"copy": V.tensor_copy, "tt": V.tensor_tensor, "ts": V.tensor_scalar, "set": V.memset, "tr": V.transpose,
             "scan": V.tensor_tensor_scan, "q": V.quantize_mx, "act": g.scalar.activation, "mx": g.tensor.matmul_mx,
             "iota": lambda *a: g.iota(*a, allow_small_or_imprecise_dtypes=True), "iota32": g.iota}

    def do(q, name, args, soft=()):
        k = 2 if name == "q" else 1
        fn = lambda: calls[name](*[mat(a) if _isop(a) else a for a in args])
        return add(q, fn, args[:k], [a for a in args[k:] if _isop(a)], _cost(name.replace("32", ""), args), 0.0, "own", (), soft)

    v = lambda name, *args, soft=(): do("v", name, args, soft)
    act = lambda *args, soft=(): do("s", "act", args, soft)
    mx = lambda *args: do("t", "mx", args)
    iota = lambda *args: do("p", "iota", args)

    def dma(q, sem, out, in_, outs, ins, extra=(), lat=2.1):
        e = {"y": g.sync, "s": g.scalar}[q]
        total[sem] = total.get(sem, 0) + 16
        return add(q, lambda: e.dma_start(out(), in_()), outs, ins, 0.06, lat, sem, extra)

    def send(dst, out, in_, sem, *more):
        c = T.cores[dst]
        rid, pid, _ = topo.addr(c)
        total["sent"] = total.get("sent", 0) + len(topo.engines(core, c))
        i = add("p", lambda: g.remote_dma(mat(out), mat(in_), T.sem[sem], T.sem["sent"], pid, rid, topo.mask(core, c)), [], [in_] + list(more), 0.25)
        ops[i]["n"] = _width(in_) * BYTES[SCRATCH[in_[1]][2]]
        return i

    def arrive(sem, src, writes, outs, lat, extra):
        total[sem] = total.get(sem, 0) + writes * sum(len(topo.engines(T.cores[s], core)) for s in src)
        return add(None, None, outs, [], 0.0, lat, sem, extra)

    def pick(to, a, z, win, c, d, off):
        act(_o(to + "s", a, z), _ind(_o(win + "s", c, d), off), F.Copy)
        return v("copy", _cast(_o(to, a, z), "u32"), _ind(_cast(_o(win, c, d), "u32"), off))

    o = _o
    f = lambda k: _o("sf", k, k + 1)
    ps = lambda b, n, a=0: _o("ps", 512 * b + a, 512 * b + a + n)
    blk = lambda x, e: _part(x, 32 * e)
    half = lambda x, h: _part(x, 64 * h, 64)
    fill = lambda out, x: act(out, o("i16", 0, _width(out))[:7] + out[7:], F.Identity, x, 0.0)

    def move(n, out, in_):
        return v("copy", out, in_) if n % 2 == 0 else act(out, in_, F.Copy)

    dr = dma("s", "dr", lambda: T.rtt[:, 0:16], lambda: T.rt[:, 0:16], [o("rtt", 0, 16)], [])
    dma("y", "dx", lambda: T.xt[:, 0:512], lambda: T.x[:, 0:512], [o("xt", 0, 512)], [], (), 2.6)
    dma("y", "dx2", lambda: T.xt[:, 512:896], lambda: T.x[:, 512:896], [o("xt", 512, 896)], [], (), 3.0)
    dma("y", "dw", lambda: T.wt[:, :], lambda: T.w[:, :], [o("wt")], [], (dr,), 4.0)
    dma("y", "du", lambda: T.ut[:, :], lambda: T.u[:, :], [o("ut")], [], (dr,), 4.4)
    dma("y", "dv", lambda: T.vt[:, :], lambda: T.v[:, :], [o("vt")], [], (dr,), 4.8)

    do("p", "iota32", (o("si", 0, 1), [[0, 1]], 0, 1))
    do("p", "iota32", (o("sj", 0, 8), [[1, 4], [0, 2]], 124, 0))
    do("p", "iota32", (o("sj", 20, 32), [[1, 6], [0, 2]], 1, 0))
    iota(o("kl0"), [[256, 8]], 0, 0)
    iota(o("i16"), [[0, 16], [1, 16]], 0, 0)
    iota(o("i3"), [[0, 224], [1, 3]], 0, 0)
    v("set", o("rtt", 16, 496), 0.0)
    v("set", o("xt", 896, 1024), 0.0)
    v("set", o("ul"), 0)
    v("ts", o("sj", 8, 20), o("sj", 20, 32), 3, None, A.bitwise_and)
    v("copy", o("sl"), o("sj", 0, 20))
    v("ts", o("si", 1, 2), o("si", 0, 1), 15, None, A.bitwise_and)
    v("ts", o("si", 2, 3), o("si", 0, 1), 5, None, A.logical_shift_right)
    v("ts", o("si", 3, 4), o("si", 0, 1), 16, 4, A.bitwise_and, A.logical_shift_right)
    v("copy", o("sf", 0, 3), o("si", 1, 4))
    for i in (1, 2, 3):
        v("ts", f(15 + i), f(1), 3.5 - i, -1e-30, A.is_gt, A.mult)
    v("ts", o("sf", 19, 22), o("sf", 16, 19), 2.0, 1e-30, A.mult, A.add)
    v("ts", f(8), f(0), 16.0, None, A.mult)
    v("ts", o("klo"), o("kl0"), f(8), None, A.add)
    v("ts", o("khi"), o("kl0"), f(8), 16.0, A.add, A.add)
    v("ts", o("bt", 0, 912, 114), o("khi"), -128.0, None, A.mult)
    v("ts", o("bt", 1, 912, 114), o("khi"), 16.0, None, A.mult)
    v("set", o("rsl"), 1.0)
    v("set", o("rsl", 0, 912, 114), 0.0)
    for k, x in ((0, 4.0), (1, -BIG), (3, 3.5), (4, -BIG), (5, 0.0), (7, BIG / 2)):
        v("set", o("d0", k, 896, 8), x)
    for k, x in ((0, BIG), (3, BIG), (4, 0.0), (7, -BIG / 2)):
        v("set", o("d1", k, 896, 8), x)
    act(o("rst3"), o("i3"), F.Sign)
    act(o("rst16"), o("i16"), F.Sign)
    act(f(4), f(0), F.Identity, 0.0, -1.0)
    act(o("mk0"), o("i16"), F.Abs, f(4))
    act(o("mask"), o("mk0"), F.Relu, 1.0, -1.0)
    act(f(3), f(2), F.Identity, 1.0, -1.0)
    for k in range(3):
        act(f(9 + k), f(0), F.Identity, float(16 * k))
    act(f(12), f(1), F.Identity, -1.0, 128.0)
    for e in every:
        fill(blk(f(13), e), float(-1 - 128 if e == me else 144 + 48 * others.index(e) - 1 - 128))
    act(f(14), f(1), F.Identity, 99.0, -1.0)
    act(f(15), f(1), F.Identity, 1.0, 2.0)
    fill(o("one"), 1.0)
    fill(o("rs2", 0, 192), 1.0)
    fill(o("rs2", 192, 384), 1.0)
    fill(o("rs2", 0, 384, 128), 0.0)
    for x in (o("zero"), o("wnw"), o("zr", 224, 240), o("wsc", 672, 688), o("hb", 512, 576), o("cn")):
        fill(x, 0.0)
    fill(o("gt", 512, 520), -9e29)
    fill(o("gt", 520, 528), 9e29)

    v("ts", o("rtt", 496, 512), o("rtt", 0, 16), -1.0, None, A.mult)
    v("q", o("rq"), o("rqs"), o("rtt", 0, 512))
    pick("rr", 0, 128, "rq", 0, 128, o("sl", 0, 8))
    pick("rr", 128, 256, "rq", 0, 128, o("sl", 8, 16))
    pick("rr", 256, 320, "rq", 0, 128, o("sl", 16, 20))
    spot = [("d1", 1), ("d0", 2), ("d1", 2)]
    for h, n in enumerate((128, 96)):
        x0 = 128 * h
        v("q", o("xq", x0, x0 + 128), o("xqs", x0, x0 + 128), o("xt", 4 * x0, 4 * x0 + 512))
        for first in (True, False):
            for i in range(3):
                lo = 0 if first else 128 + 32 * i
                mx(ps(3 * h + i, 128), o("rr", lo, lo + 128), o("rrs", lo, lo + 128), o("xq", x0, x0 + 128), o("xqs", x0, x0 + 128), first, not first)
        for i, (name, k) in enumerate(spot):
            v("ts", o(name, 4 * x0 + k, 4 * (x0 + n), 4), ps(3 * h + i, n), f(16 + i), 3.0, A.is_le, A.mult)
        s = (4 * x0, 4 * (x0 + n))
        v("scan", o("uu", *s), o("d0", *s), o("d1", *s), o("uu", 511, 512) if h else 0.0, A.add, A.add)
    for c in range(8):
        v("ts", o("bt", 114 * c + 2, 114 * c + 114), o("uu", 7, 896, 8), o("klo", c, c + 1), o("khi", c, c + 1), A.max, A.min)
    v("scan", o("sc"), o("rsl"), o("bt"), 0.0, A.mult, A.subtract)
    counts = o("sc", 113, 912, 114)

    sent = []
    for e in every:
        for b in range(4):
            v("ts", blk(o("off2", 8 * e, 8 * e + 8), b), blk(counts, e), 0.125, None, A.mult)
        last = pick("xs", 128 * e, 128 * e + 128, "xq", 0, 256, o("off2", 8 * e, 8 * e + 8))
        if e != me:
            after = [last]
            i = place(me, e)
            sent.append(send(e, _cast(o("xl", 128 * i, 128 * i + 128), "u8"), _cast(o("xs", 128 * e, 128 * e + 128), "u8"), "xa%d" % i))
            sent.append(send(e, o("xls", 128 * i, 128 * i + 128), o("xss", 128 * e, 128 * e + 128), "xa%d" % i, o("xs", 128 * e, 128 * e + 128)))

    for h, n in enumerate((128, 96)):
        for i in range(3):
            act(o("sg", 384 * h + i, 384 * h + 3 * n, 3), ps(3 * h + i, n), F.Sign, f(19 + i), -1.0)

    for i in range(4):
        v("q", o("wq", 128 * i, 128 * i + 128), o("wqs", 128 * i, 128 * i + 128), o("wt", 512 * i, 512 * i + 512), soft=after)
    v("q", o("uq"), o("uqs"), o("ut"), soft=after)
    pick("ur", 0, 128, "uq", 0, 128, o("ul"))

    def chunk(xc, lo, hlo, hn, hc, hto, banks, b):
        for i, k in enumerate(banks):
            mx(ps(k, 128), o("wq", 128 * i, 128 * i + 128), o("wqs", 128 * i, 128 * i + 128), o(xc, lo, lo + 128), o(xc + "s", lo, lo + 128), True, True)
            out = o("hb", hlo + i, hlo + 512, 4)
            if i % 2 == 0 or hc == "zq":
                act(out, ps(k, 128), F.Relu, 0.0, 0.0625)
            else:
                v("ts", out, ps(k, 128), 0.0, 0.0625, A.max, A.mult)
        v("q", o(hc, hto, hto + hn), o(hc + "s", hto, hto + hn), o("hb", hlo, hlo + 4 * hn))
        mx(ps(b, 128), o("ur"), o("urs"), o(hc, hto, hto + 128), o(hc + "s", hto, hto + 128), True, True)

    asked = []
    BANKS = [((6, 7, 0, 1), 2), ((3, 4, 5, 6), 7), ((0, 1, 2, 3), 4)]
    for n, s in enumerate(order):
        i = others.index(s)
        arrive("xa%d" % i, [s], 2, [o("xl", 128 * i, 128 * i + 128), o("xls", 128 * i, 128 * i + 128)], 2.3, sent[2 * n:2 * n + 2])
        chunk("xl", 128 * i, 576 + 512 * i, 128, "hq", 128 * i, *BANKS[n])
        for h in range(2):
            v("tr", half(o("qs", 64 * i, 64 * i + 64), h), half(ps(BANKS[n][1], 64, 64 * h), h))
        k = place(me, s)
        asked.append(send(s, o("ql", 4 * k, 4 * k + 2), o("qs", 64 * i + 31, 64 * i + 33), "qa%d" % k))

    chunk("xs", 128 * me, 0, 144, "zq", 0, (5, 6, 7, 0), 1)
    act(o("gt", 128 * me, 128 * me + 128), ps(1, 128), F.Copy)
    act(blk(o("qo"), me), blk(ps(1, 128), me), F.Copy)

    for h, n in enumerate((128, 96)):
        s = (384 * h, 384 * h + 3 * n)
        v("scan", o("wsc", *s), o("rst3", *s), o("sg", *s), 0.0, A.mult, A.add, soft=after)
    v("ts", o("nn"), o("wsc", 2, 672, 3), 0.0, None, A.is_gt)
    v("scan", o("pp"), o("one"), o("nn"), 0.0, A.mult, A.add)
    for s in ((0, 112), (112, 224)):
        v("tt", o("zr", *s), o("nn", *s), o("pp", *s), A.mult)
    v("ts", o("ea", 0, 16), o("off2", 0, 32, 2), f(3), None, A.mult, soft=after)
    v("ts", o("ea", 16, 32), o("off2", 1, 32, 2), f(2), None, A.mult, soft=after)
    v("tt", o("ea", 32, 48), o("ea", 0, 16), o("ea", 16, 32), A.add)
    for k in range(2):
        v("copy", o("offe", k, 32, 2), o("ea", 32, 48))
    for e in range(4):
        act(o("gz", 128 * e, 128 * e + 128), _ind(o("zr"), o("offe", 8 * e, 8 * e + 8)), F.Copy)
    for s in ((0, 256), (256, 512)):
        v("tr", o("gs", *s), o("gz", *s))
    gw = o("gs", 0, 512, 16)
    v("ts", o("ga"), gw, 128.5, 1024.0, A.is_gt, A.mult)
    v("ts", o("gd"), gw, 0.5, None, A.is_gt)
    v("tt", o("gb"), gw, o("ga"), A.add)
    v("ts", o("gc"), o("gb"), f(12), 512.0, A.add, A.min)
    v("tt", o("gx"), o("gc"), o("gd"), A.mult)
    for e in every:
        for k, b in enumerate([r for r in every if r != e]):
            move(1 if k else 0, blk(o("gy", 8 * k, 8 * k + 8), e), blk(o("gx", 8 * e, 8 * e + 8), b))
    v("tt", o("gp", 0, 8), o("gy", 0, 8), o("gy", 8, 16), A.add)
    v("tt", o("gp", 8, 16), o("gp", 0, 8), o("gy", 16, 24), A.add)
    v("ts", o("ol3"), counts, 0.375, 2.0, A.mult, A.add, soft=after)
    v("tt", o("wg"), _ind(o("wsc"), o("ol3")), o("mask", 0, 128), A.mult)
    v("scan", o("ws"), o("rst16", 0, 128), o("wg"), 0.0, A.mult, A.add)
    for k in range(2):
        v("ts", o("gm", 8 * k, 8 * k + 8), o("ws", 15, 128, 16), 3.0 - 2 * k, 520.0, A.not_equal, A.mult)
        v("tt", o("gl", 8 * k, 8 * k + 8), o("gm", 8 * k, 8 * k + 8), o("gp", 8, 16), A.max)
    v("copy", o("offl"), o("gl"))

    for n, e in enumerate(order):
        i = others.index(e)
        arrive("qa%d" % i, [e], 1, [o("ql", 4 * i, 4 * i + 2)], 1.6, asked[n:n + 1])
        v("ts", o("rep", 64 * i, 64 * i + 32), o("zero"), o("ql", 4 * i, 4 * i + 1), None, A.add)
        act(o("rep", 64 * i + 32, 64 * i + 64), o("zero"), F.Identity, o("ql", 4 * i + 1, 4 * i + 2))
        for h in range(2):
            for to in range(2):
                v("tr", half(o("gt", 128 * e + 64 * h, 128 * e + 64 * h + 64), to), half(o("rep", 64 * i, 64 * i + 64), h))
            if n == 2:
                v("tr", blk(o("qo", 64 * h, 64 * h + 64), e), blk(o("rep", 64 * i, 64 * i + 64), 2 * h))
        if n < 2:
            act(blk(o("qo"), e), blk(o("gt", 128 * e, 128 * e + 128), e), F.Copy)
    v("tt", o("a1", 0, 128), _ind(o("gt"), o("offl", 0, 8)), o("qo"), A.is_le)
    v("tt", o("a1", 128, 256), _ind(o("gt"), o("offl", 8, 16)), o("qo"), A.is_lt)
    v("scan", o("a2"), o("a1", 0, 128), o("a1", 128, 256), 0.0, A.add, A.add)
    for k in range(3):
        v("ts", o("bt2", 128 * k, 128 * k + 128), o("a2"), f(9 + k), None, A.is_le)
    v("scan", o("sc2"), o("rs2"), o("bt2"), 0.0, A.mult, A.add)
    told, made = [], []
    for n, e in enumerate(order):
        for b in range(4):
            made.append(v("ts", blk(o("ls", 4 * e, 4 * e + 3), b), blk(o("sc2", 127, 384, 128), e), 127.0, None, A.min))
        i = place(me, e)
        told.append(send(e, o("la", 4 * i, 4 * i + 3), o("ls", 4 * e, 4 * e + 3), "ar%d" % i))

    v("tt", o("zm"), o("zr", 0, 224), o("mask", 0, 224), A.mult, soft=made)
    v("scan", o("zs2"), o("rst16", 0, 224), o("zm"), 0.0, A.mult, A.add)
    v("copy", o("offp"), o("zs2", 15, 224, 16))
    v("q", o("vq"), o("vqs"), o("vt"), soft=made)
    v("tt", o("a3"), o("a1", 0, 128), o("a1", 128, 256), A.add, soft=made)
    v("tt", o("cn", 1, 129), o("a3"), o("a2"), A.mult)
    v("tt", o("g2"), _ind(o("cn"), o("offp")), o("mask", 0, 224), A.mult)
    v("scan", o("g3"), o("rst16", 0, 224), o("g2"), 0.0, A.mult, A.add)
    rk = o("g3", 15, 224, 16)
    v("ts", o("won"), rk, 0.5, None, A.is_gt)
    v("ts", o("h1"), rk, 48.5, None, A.is_lt)
    v("ts", o("xz"), rk, f(13), None, A.add)
    v("ts", blk(o("xz"), me), blk(o("zs2", 15, 224, 16), me), blk(f(13), me), None, A.add)
    v("tt", o("hm"), o("won"), o("h1"), A.mult)
    v("ts", o("w1"), o("won"), f(14), None, A.mult)
    v("tt", o("zw", 0, 14), o("hm"), o("xz"), A.mult)
    v("ts", o("w2"), o("hm"), f(15), None, A.mult)
    v("tt", o("zw", 14, 28), o("w1"), o("w2"), A.add)
    for h in range(2):
        move(h, half(o("t1"), h), half(o("zw"), 1 - h))
    v("tt", o("s1"), o("zw"), o("t1"), A.add)
    for b in range(4):
        move(b, blk(o("t2"), b), blk(o("s1"), b ^ 1))
    v("tt", o("s2"), o("s1"), o("t2"), A.add)
    v("ts", o("off5"), o("s2", 0, 14), 128.0, None, A.add)
    v("ts", blk(o("wnw", 0, 14), 0), blk(o("s2", 14, 28), 0), -100.0, None, A.add)
    v("tr", blk(o("wnf"), 0), blk(o("wnw"), 0))
    dma("y", "out", lambda: T.wn[:, :], lambda: T.wnf[0:14, 0:16], [], [blk(o("wnf"), 0)])

    came = []
    for n, s in enumerate(order):
        i = others.index(s)
        arrive("ar%d" % i, [s], 1, [o("la", 4 * i, 4 * i + 3)], 1.6, told[n:n + 1])
        pick("hs", 48 * i, 48 * i + 48, "hq", 128 * i, 128 * i + 128, o("la", 4 * i, 4 * i + 3))
        k = 144 + 48 * place(me, s)
        came.append(send(s, _cast(o("zq", k, k + 48), "u8"), _cast(o("hs", 48 * i, 48 * i + 48), "u8"), "ha"))
        came.append(send(s, o("zqs", k, k + 48), o("hss", 48 * i, 48 * i + 48), "ha", o("hs", 48 * i, 48 * i + 48)))

    arrive("ha", others, 2, [o("zq", 144, 288), o("zqs", 144, 288)], 1.8, came)
    pick("z", 0, 128, "zq", 0, 288, o("off5", 0, 8))
    pick("z", 128, 224, "zq", 0, 288, o("off5", 8, 14))
    mx(ps(0, 128), o("vq"), o("vqs"), o("z", 0, 128), o("zs", 0, 128), True, True)
    mx(ps(1, 128), o("vq"), o("vqs"), o("z", 96, 224), o("zs", 96, 224), True, True)
    v("copy", o("ysb", 0, 128), ps(0, 128))
    v("copy", o("ysb", 128, 224), o("ps", 544, 640))
    dma("y", "out", lambda: T.oc[:, :], lambda: T.z[:, 0:224].bitcast(dt.uint8), [], [o("z")])
    for k in range(4):
        dma("s" if k % 2 == 0 else "y", "out", lambda k=k: T.osc[4 * k:4 * k + 4, :], lambda k=k: T.zs[32 * k:32 * k + 4, :], [], [o("zs")])
    for a, z in ((0, 128), (128, 224)):
        dma("s" if a else "y", "out", lambda a=a, z=z: T.y[:, a:z], lambda a=a, z=z: T.ysb[:, a:z], [], [o("ysb", a, z)])

    queue = {"v": V, "s": g.scalar, "t": g.tensor, "p": g, "y": g.sync}
    lists = _order(ops)
    mark = {}
    for q, items in lists.items():
        n = 0
        for i in items:
            if ops[i]["sem"] == "own":
                n += 1
                mark[i] = (q, n)
        total[q] = n
    for i, x in enumerate(ops):
        if x["sem"] and x["sem"] != "own":
            mark[i] = (x["sem"], total[x["sem"]])
    seen = {}
    for q, items in lists.items():
        for i in items:
            best = {}
            for d in ops[i]["deps"]:
                if d in mark and not (q == "t" and ops[d]["q"] == "t"):
                    s, n = mark[d]
                    best[s] = max(n, best.get(s, 0))
            for s, n in sorted(best.items()):
                if seen.get((q, s), 0) < n:
                    queue[q].wait_ge(T.sem[s], n)
                    seen[(q, s)] = n
            call = ops[i]["fn"]()
            if ops[i]["sem"]:
                call.then_inc(T.sem[mark[i][0]], 1 if ops[i]["sem"] == "own" else 16)
    for s, n in sorted(total.items()):
        if n and seen.get(("p", s), 0) < n:
            g.wait_ge(T.sem[s], n)
